import numpy as np, ml_dtypes
CORES = [35,38,43,46]
N = 4
BF = ml_dtypes.bfloat16
def gentries(a):
    return np.ascontiguousarray(a.reshape(8, 16, -1).transpose(0, 2, 1)).reshape(8, -1)
def gtable(e):
    e = np.asarray(e); return np.ascontiguousarray(e.reshape(8, -1, 16).transpose(0, 2, 1)).reshape(128, -1).astype(np.int32)
W, L, T, TH, A, B, FO = 4096, 256, 8, 60, 4, 10, 8
def parts(rng):
    return (rng.integers(0, 16, (N, 8, 16, W)), rng.integers(0, W, (N, 8, 16, W)), rng.integers(0, 64, (N, 8, 16, L)), rng.integers(0, W, (N, 8, 16, L)),
            rng.integers(0, W, (N, 8, 16, L)), rng.integers(0, 16, (N, 8, 16, L)), rng.integers(0, W, (N, 8, L)), rng.integers(0, 64, (N, 8, 16)))
def keys(x, w, p):
    z = np.take_along_axis(x, p[:, :, None, :], 3)
    return np.add.reduce(z * w[..., None], axis=2) & 63
def pack(x, d, m, u, n, q, o, w):
    return {"feat": np.ascontiguousarray(x.reshape(N, 128, W)).astype(np.float32).astype(BF), "kids": np.ascontiguousarray(d.reshape(N, 128, W)).astype(np.int32),
            "mkey": np.ascontiguousarray(m.reshape(N, 128, L)).astype(np.float32).astype(BF), "mobj": np.ascontiguousarray(u.reshape(N, 128, L)).astype(np.int32),
            "cand": np.stack([gtable(a.transpose(0, 2, 1).reshape(8, -1)) for a in n]), "want": np.ascontiguousarray(q.reshape(N, 128, L)).astype(np.float32).astype(BF),
            "last": np.ascontiguousarray(o).astype(np.int32), "wts": np.ascontiguousarray(w.reshape(N, 128, 1)).astype(np.int32)}
def setup_inputs(rng):
    return pack(*parts(rng))
def setup_inputs_corners(rng):
    x, d, m, u, n, q, o, w = parts(rng); own = np.arange(W)[None, None, None, :]
    kind = rng.integers(0, 7, (N, 8, 1, W))
    d = np.where(kind == 0, own, d); d = np.where(kind == 1, (own + 1) % W, d)
    d = np.where(kind == 2, (W - 1) * rng.integers(0, 2, d.shape), d); d = np.where(kind == 3, d[:, :, :1, :], d)
    d[2] = d[2] & -2
    x[3, :, 0] = (x[3, :, 0] & 14) | (own[0, 0] & 1); w[3] = w[3] & 62; w[3, :, 0] = w[3, :, 0] | 1
    p = rng.integers(0, W, (N, 8, L)); p[1] = 1 + np.argsort(rng.random((8, W - 2)), axis=1)[:, :L]
    p[:, :, 0] = 0; p[:, :, L - 1] = W - 1; p[3] = p[3] | 1
    n0 = n[0]; n = np.repeat(p[:, :, None, :], 16, axis=2); n[0] = np.where(rng.random((8, 1, L)) < 0.5, n0, n[0])
    j = rng.choice(np.array([0, A - 1, A, B - 1, B, 15, 16]), (N, 8, L))
    j[1] = np.where(j[1] == 16, 15, j[1]); j[2] = 16; j[3] = np.where(j[3] == 16, 0, j[3]); j[3, 7, L - 1] = 16
    c = keys(x, w, p)[:, :, None, :]; rows = np.arange(16)[None, None, :, None]; jj = j[:, :, None, :]
    off = rng.integers(1, 64, m.shape); off[3] = 2 * rng.integers(1, 32, off[3].shape)
    m = np.where((rows == jj) | ((rows > jj) & (rng.random(m.shape) < 0.2)), c, (c + off) & 63)
    m[1, :, :, 1] = c[1, :, :, 1]
    s = rng.integers(0, 5, u.shape); u = np.where(s == 0, 0, np.where(s == 1, W - 1, np.where(s == 2, p[:, :, None, :], u)))
    s = rng.integers(0, 4, o.shape); o = np.where(s == 0, 0, np.where(s == 1, W - 1, np.where(s == 2, p, o)))
    u[1, :, :, 1] = rng.integers(1, W - 1, (8, 16)); u[1, :, :, L - 1] = rng.integers(1, W - 1, (8, 16))
    z = np.take_along_axis(x[1], p[1][:, None, :], 2)
    q[1, 6] = z[6]; q[1, 7] = np.where(z[7] >= 8, 0, 15); u[1, 6, 0, 0] = W - 1; o[1, 6, 0] = 0
    return pack(x, d, m, u, n, q, o, w)
def setup_inputs_ends(rng):
    x, d, m, u, n, q, o, w = parts(rng)
    x = 15 * (rng.random((N, 8, 16, W)) < rng.choice(np.array([0.0, 0.3, 0.5, 0.5, 0.7, 1.0]), (N, 8, 1, W))).astype(np.int64)
    for g in range(8):
        x[:, g, :, 0] = 15 * (g & 1); x[:, g, :, W - 1] = 15 * (g & 1)
        x[:, g, :, W - 2] = 15 * (g & 1); x[:, g, 15, W - 2] = 15 - 15 * (g & 1)
    w = 63 * rng.integers(0, 2, w.shape); w[:, 6:] = 63; w[:, 0] = 0
    q = 15 * rng.integers(0, 2, q.shape)
    d = np.where(rng.random(d.shape) < 0.7, (W - 1) * rng.integers(0, 2, d.shape), d)
    n = np.where(rng.random(n.shape) < 0.7, (W - 1) * rng.integers(0, 2, n.shape), n)
    u = np.where(rng.random(u.shape) < 0.7, (W - 1) * rng.integers(0, 2, u.shape), u)
    o = np.where(rng.random(o.shape) < 0.75, (W - 1) * rng.integers(0, 2, o.shape), o)
    m = np.where(rng.random(m.shape) < 0.7, 63 * rng.integers(0, 2, m.shape), (49 * rng.integers(0, 17, m.shape)) & 63)
    for l in (0, 1, 2, 3, L - 4, L - 3, L - 2, L - 1): n[:, :, 0::2, l] = W - 1; n[:, :, 1::2, l] = 0
    for l, k in ((2, 1), (3, 13), (L - 4, 1), (L - 3, 13)): n[:, :, k, l] = W - 2; n[:, :, 14, l] = W - 2
    for g in range(8):
        for l in (1, 2, 3, L - 4, L - 3, L - 1): q[:, g, :, l] = 15 - 15 * (g & 1)
        for l in (0, L - 2): q[:, g, :, l] = 15 * (g & 1)
    kk = keys(x, w, np.full((N, 8, 1), W - 1))
    m[:, :, 12:, L - 1] = 63; u[:, :, 12:, L - 1] = W - 1
    m[:, :, 11, 1] = kk[:, :, 0]; m[:, :, 11, L - 1] = kk[:, :, 0]
    h = W // FO
    d[:, 7, 15, h - 1::h] = W - 1; d[:, 7, 15, h - 2::h] = W - 1; d[:, :, 0, 0::h] = 0
    return pack(x, d, m, u, n, q, o, w)
def setup_inputs_shared(rng):
    x, d, m, u, n, q, o, w = parts(rng)
    hot = np.stack([np.concatenate([np.array([0, W - 1]), 1 + rng.permutation(W - 2)[:22]]) for g in range(8)])
    gg = np.arange(8)[None, :, None, None]
    d = hot[gg, rng.integers(0, 24, d.shape)]; n = hot[gg, rng.integers(0, 24, n.shape)]
    u = np.where(rng.random(u.shape) < 0.5, hot[gg, rng.integers(0, 24, u.shape)], u)
    kh = keys(x, w, np.repeat(hot[None], N, axis=0))
    m = np.where(rng.random(m.shape) < 0.6, kh[np.arange(N)[:, None, None, None], gg, rng.integers(0, 24, m.shape)], m)
    for r, g, i in ((0, 0, 2), (N - 1, 7, 1)):
        n[r, g] = hot[g, i]; m[r, g, 0] = kh[r, g, i]; u[r, g, 0, 0] = hot[g, 3]
    return pack(x, d, m, u, n, q, o, w)
def setup_inputs_spread(rng):
    x, d, m, u, n, q, o, w = parts(rng)
    def uneven(top, shape, kshape):
        return np.minimum((top * rng.random(shape) ** np.exp2(rng.integers(-2, 3, kshape))).astype(np.int64), top - 1)
    x = uneven(16, x.shape, (N, 8, 1, W)); q = uneven(16, q.shape, (N, 8, 1, L)); d = uneven(W, d.shape, (N, 8, 16, 1))
    u = uneven(W, u.shape, (N, 8, 1, L)); n = uneven(W, n.shape, (N, 8, 16, 1)); o = uneven(W, o.shape, (N, 8, 1)); w = uneven(64, w.shape, (N, 8, 1))
    m = m & rng.choice(np.array([63, 63, 7, 56, 1]), (N, 8, 1, L))
    return pack(x, d, m, u, n, q, o, w)
def setup_inputs_ties(rng):
    x, d, m, u, n, q, o, w = parts(rng); h = W // 2
    x[..., h:] = x[..., :h][..., ::-1]
    p = rng.integers(0, W, (N, 8, L)); p[:, :, L - 1] = W - 1
    z = np.take_along_axis(x, p[:, :, None, :], 3); tot = TH + rng.integers(-1, 2, (N, 8, 1, L))
    dl = (tot >> 4) + (np.arange(16)[None, None, :, None] < (tot & 15))
    q = np.where(z >= 8, z - dl, z + dl)
    twin = np.where(rng.random(n.shape) < 0.5, p[:, :, None, :], W - 1 - p[:, :, None, :])
    n = np.where(rng.random(n.shape) < 0.6, twin, n)
    c = keys(x, w, p)[:, :, None, :]
    m = np.where(rng.random((N, 8, 1, L)) < 0.4, (c + (m & 3)) & 63, m)
    return pack(x, d, m, u, n, q, o, w)
def check_inputs(d):
    bad = []
    for k, lo, hi in (("feat", 0, 15), ("kids", 0, W - 1), ("mkey", 0, 63), ("mobj", 0, W - 1), ("cand", 0, W - 1), ("want", 0, 15), ("last", 0, W - 1), ("wts", 0, 63)):
        v = np.asarray(d[k]).astype(np.float64)
        if not (np.min(v) >= lo and np.max(v) <= hi and np.all(v == np.rint(v))): bad.append("range of " + k)
    return bad
def reference(feat, kids, mkey, mobj, cand, want, last, wts):
    x = np.ascontiguousarray(feat.astype(np.int32).reshape(N, 8, 16, W).transpose(0, 1, 3, 2))
    d = np.array(kids.astype(np.int64).reshape(N, 8, 16, W).transpose(0, 1, 3, 2))
    m = np.array(mkey.astype(np.int64).reshape(N, 8, 16, L).transpose(0, 1, 3, 2))
    u = np.array(mobj.astype(np.int64).reshape(N, 8, 16, L).transpose(0, 1, 3, 2))
    n = np.stack([gentries(a) for a in cand]).astype(np.int64).reshape(N, 8, L, 16)
    q = np.array(want.astype(np.int32).reshape(N, 8, 16, L).transpose(0, 1, 3, 2))
    prev = np.array(last.astype(np.int64)); w = wts.astype(np.int64).reshape(N, 8, 1, 16)
    count = np.zeros(N, np.int64); gi = np.arange(8)[:, None]
    for t in range(T):
        seen = np.zeros(N, np.int64)
        for r in range(N):
            s = (r + t) % N
            dist = np.add.reduce(np.abs(x[s][gi[:, :, None], n[r]] - q[r][:, :, None, :]), axis=3)
            like = dist < TH + (count[s] & 15); alike = np.any(like, axis=2)
            k = np.where(alike, np.argmax(like, axis=2), np.argmin(dist, axis=2))
            o = np.take_along_axis(n[r], k[:, :, None], 2)[:, :, 0]
            xo = x[s][gi, o]; c = np.add.reduce(xo * w[s], axis=2) & 63
            hit = m[s] == c[:, :, None]; covered = np.any(hit, axis=2); j = np.argmax(hit, axis=2)
            own = d[s][gi, o]; e = d[s][gi, np.take_along_axis(u[s], j[:, :, None], 2)[:, :, 0]]
            top = covered & (j < B); low = covered & ((j < A) | (j >= B))
            new = np.concatenate([np.where(top[:, :, None], e[:, :, :8], own[:, :, :8]), np.where(low[:, :, None], e[:, :, 8:], own[:, :, 8:])], axis=2)
            g, l = np.nonzero(covered); first = np.unique(g * W + o[g, l], return_index=True)[1]
            g, l = g[first], l[first]; d[s, g, o[g, l]] = new[g, l]
            g, l = np.nonzero(~alike); row = (l + 5 * t) & 15
            m[s, g, l, row] = c[g, l]; u[s, g, l, row] = prev[r, g, l]
            seen[s] = np.count_nonzero(covered); prev[r] = o; n[r] = new; q[r] = np.abs(q[r] - xo)
        count = seen
    dd = d.transpose(0, 1, 3, 2).reshape(N, 128, FO, W // FO)
    return {"yn": n.transpose(0, 1, 3, 2).reshape(N, 128, L).astype(np.float32), "ymu": (64 * u + m).transpose(0, 1, 3, 2).reshape(N, 128, L).astype(np.float32),
            "yd": np.add.reduce(dd * np.arange(1, FO + 1)[:, None], axis=2).astype(np.float32)}

@@ -1,0 +1,424 @@
+from concourse.mybir import AluOpType as ALU, AxisListType, ActivationFunctionType as AF
+
+STEPS, W, L, LIM = 8, 4096, 256, 60
+CH = [(0, 4), (4, 8), (8, 12), (12, 14), (14, 16)]
+KD = 6
+BIG = float(2 ** 26)
+
+_f, _b, _h, _i, _u = "float32", "bfloat16", "float16", "int32", "uint16"
+SCRATCH = {
+    "featW": ("sbuf", [128, 2 * W], _b), "kidi": ("sbuf", [128, W], _i), "kid": ("sbuf", [128, W + 16], _f),
+    "keyW": ("sbuf", [128, W], _f), "idW": ("sbuf", [128, W + 16], _f),
+    "Wx": ("sbuf", [128, W], _b), "D": ("sbuf", [128, W], _b), "A": ("sbuf", [128, 16, 256], _b),
+    "LH": ("sbuf", [128, 2048], _b), "SH": ("sbuf", [128, 2048], _h), "R16": ("sbuf", [128, 8, 32], _h),
+    "i1": ("sbuf", [128, 128], _i), "i1b": ("sbuf", [128, 128], _i), "i2": ("sbuf", [128, 256], _i), "i2b": ("sbuf", [128, 256], _i),
+    "i3": ("sbuf", [128, 256], _i), "i3b": ("sbuf", [128, 256], _i), "i4": ("sbuf", [128, 16], _i), "i5": ("sbuf", [128, 8], _i),
+    "i6": ("sbuf", [128, 256], _i), "ib": ("sbuf", [128, 8], _i),
+    "blk": ("sbuf", [128, 128], _f), "diag": ("sbuf", [128, 256], _f), "I16": ("sbuf", [128, 128], _h), "IB": ("sbuf", [128, 128], _b),
+    "IN": ("sbuf", [128, 128], _b), "If": ("sbuf", [128, 128], _f), "ones": ("sbuf", [128, 128], _b), "wblk": ("sbuf", [128, 128], _b),
+    "b8": ("sbuf", [128, 8], _b), "Kc": ("sbuf", [128, 256], _h), "expl": ("sbuf", [128, 16], _u),
+    "RST": ("sbuf", [128, 256], _f), "RZ": ("sbuf", [128, 256], _f), "R1": ("sbuf", [128, 256], _f), "R2": ("sbuf", [128, 256], _f),
+    "CJ": ("sbuf", [128, 256], _f), "CJ2": ("sbuf", [128, 256], _f), "t1": ("sbuf", [128, 256], _f), "t2": ("sbuf", [128, 256], _f), "t3": ("sbuf", [128, 256], _f),
+    "col": ("sbuf", [128, 16], _f), "offc": ("sbuf", [128, 16], _f), "wti": ("sbuf", [128, 1], _i), "wtf": ("sbuf", [128, 1], _f),
+    "ci": ("sbuf", [128, 256], _i), "mkb": ("sbuf", [128, 256], _b), "moi": ("sbuf", [128, 256], _i), "mk16": ("sbuf", [128, 256], _h), "mo16": ("sbuf", [128, 256], _h),
+    "lai": ("sbuf", [128, 16], _i), "LX": ("sbuf", [128, 32], _f), "LT": ("sbuf", [128, 32], _f), "prev0": ("sbuf", [128, 16], _f),
+    "X": ("sbuf", [128, 16, 32], _h), "XT": ("sbuf", [128, 16, 32], _h), "Y": ("sbuf", [128, 16, 32], _h), "YT": ("sbuf", [128, 16, 32], _h),
+    "MK": ("sbuf", [128, 256], _f), "Lp": ("sbuf", [128, 256], _f), "vm": ("sbuf", [128, 256], _f), "vI": ("sbuf", [128, 256], _i),
+    "oa": ("sbuf", [128, 16], _i), "ky": ("sbuf", [128, 256], _f), "ks": ("sbuf", [128, 256], _i), "key": ("sbuf", [128, 16], _i),
+    "eq": ("sbuf", [128, 256], _f), "em": ("sbuf", [128, 256], _f), "es": ("sbuf", [128, 256], _i),
+    "eo": ("sbuf", [128, 16], _i), "sT": ("sbuf", [128, 16], _i), "sL": ("sbuf", [128, 16], _i), "de": ("sbuf", [128, 16], _i),
+    "tT": ("sbuf", [128, 16], _i), "tL": ("sbuf", [128, 16], _i), "lT": ("sbuf", [128, 16], _i), "lL": ("sbuf", [128, 16], _i),
+    "uT": ("sbuf", [128, 16], _u), "uL": ("sbuf", [128, 16], _u), "top": ("sbuf", [128, 256], _f), "cf": ("sbuf", [128, 256], _f),
+    "na": ("sbuf", [128, 16], _f), "cov": ("sbuf", [128, 16], _b), "ncd": ("sbuf", [128, 16], _f), "s1": ("sbuf", [128, 16], _f), "s1u": ("sbuf", [128, 16], _u),
+    "gl": ("sbuf", [128, 256], _f), "eq2": ("sbuf", [128, 256], _f), "dsum": ("sbuf", [128, 256], _f), "dd": ("sbuf", [128, 16], _f), "s2": ("sbuf", [128, 16], _f), "s2u": ("sbuf", [128, 32], _u),
+    "dk": ("sbuf", [128, 16], _f), "dk2": ("sbuf", [128, 16], _f), "pn": ("sbuf", [128, 16], _f), "dn": ("sbuf", [128, 16], _f), "dn2": ("sbuf", [128, 16], _f),
+    "cs": ("sbuf", [128, 1], _f), "csi": ("sbuf", [128, 1], _i), "csa": ("sbuf", [128, 1], _i), "limA": ("sbuf", [128, 1], _f), "limB": ("sbuf", [128, 1], _f),
+    "xo": ("sbuf", [128, 256], _b), "yno": ("sbuf", [128, 256], _f), "ymo": ("sbuf", [128, 256], _f), "acc": ("sbuf", [128, 512], _f),
+    "outC": ("sbuf", [128, STEPS * 272], _u), "inC": ("sbuf", [128, (STEPS + 1) * 272], _u),
+    "outW": ("sbuf", [128, STEPS * 256], _b), "inW": ("sbuf", [128, STEPS * 256], _b),
+    "pv": ("psum", [128, 512], _f), "pL": ("psum", [128, 512], _f), "pM": ("psum", [128, 512], _f), "pC": ("psum", [128, 512], _f),
+    "pW": ("psum", [128, 512], _f), "pA": ("psum", [128, 512], _f), "pB": ("psum", [128, 512], _f),
+}
+DMAS = ["cand", "want", "wts", "last", "mkey", "mobj", "f0", "fd", "k0", "k1", "k2", "k3", "yn", "ymu", "yd"]
+SEMAPHORES = ["sv", "st", "ss", "sg", "ls"] + ["d_" + n for n in DMAS] + ["w%d" % t for t in range(1, STEPS)] + ["c%d" % t for t in range(1, STEPS + 1)]
+
+
+def make(g, T):
+    Q = {"v": g.vector, "t": g.tensor, "s": g.scalar, "g": g, "y": g.sync}
+    own = {"v": "sv", "t": "st", "s": "ss", "g": "sg"}
+    cnt, known, hist, tags = {}, {q: {} for q in Q}, {}, {}
+
+    def tag(n):
+        if n not in tags:
+            tags[n] = {"w": {}, "r": {}, "base": {}, "full": False}
+        return tags[n]
+
+    def merge(a, b):
+        for s, c in b.items():
+            if a.get(s, 0) < c:
+                a[s] = c
+
+    def wait(q, needs):
+        for s in sorted(needs, key=lambda s: -len(hist.get((s, needs[s]), {}))):
+            c = needs[s]
+            if known[q].get(s, 0) < c:
+                Q[q].wait_ge(T.sem[s], c)
+                merge(known[q], hist.get((s, c), {}))
+                merge(known[q], {s: c})
+
+    def deps(q, r, w, p, acc):
+        need = {}
+        for n in r:
+            merge(need, tag(n)["w"])
+        for n in w:
+            d = tag(n)
+            for m in (d["w"], d["r"], d["base"]):
+                merge(need, {s: c for s, c in m.items() if not (acc and s == own.get(q))})
+        for n in p:
+            d = tag(n)
+            if d["full"] or d["r"]:
+                merge(d["base"], d["w"])
+                merge(d["base"], d["r"])
+                d["w"], d["r"], d["full"] = {}, {}, False
+            merge(need, d["base"])
+        return need
+
+    def mark(s, c, r, w, p, acc):
+        for n in r:
+            merge(tag(n)["r"], {s: c})
+        for n in w:
+            if acc:
+                merge(tag(n)["w"], {s: c})
+                tag(n)["r"] = {}
+            else:
+                tags[n] = {"w": {s: c}, "r": {}, "base": {}, "full": True}
+        for n in p:
+            merge(tag(n)["w"], {s: c})
+
+    def op(q, fn, args, r=(), w=(), p=(), acc=False, kw=None):
+        wait(q, deps(q, r, w, p, acc))
+        s = own[q]
+        cnt[s] = c = cnt.get(s, 0) + 1
+        fn(*args, **(kw or {})).then_inc(T.sem[s], 1)
+        hist[(s, c)] = dict(known[q])
+        mark(s, c, r, w, p, acc)
+
+    def dma(q, out, in_, name, r=(), w=(), p=()):
+        wait(q, deps(q, r, w, p, False))
+        s = "d_" + name
+        cnt[s] = 16
+        Q[q].dma_start(out, in_).then_inc(T.sem[s], 16)
+        hist[(s, 16)] = dict(known[q])
+        mark(s, 16, r, w, p, False)
+
+    def arrive(s, c, w):
+        cnt[s] = c
+        mark(s, c, (), w, (), False)
+
+    def need(q, r):
+        wait(q, deps(q, r, (), (), False))
+
+    def finish(q):
+        for s in sorted(cnt):
+            if known[q].get(s, 0) < cnt[s]:
+                Q[q].wait_ge(T.sem[s], cnt[s])
+    return op, dma, arrive, need, finish, cnt
+
+
+def rank_program(g, core, T, topo):
+    rank = T.rank_of(core)
+    if rank is None:
+        return
+    op, dma, arrive, need, finish, cnt = make(g, T)
+    v, te, sc = g.vector, g.tensor, g.scalar
+    n = len(T.cores)
+    nxt, prv = T.cores[(rank + 1) % n], T.cores[(rank - 1) % n]
+    rid, pid, _se = topo.addr(nxt)
+    mask, nout, nin = topo.mask(core, nxt), len(topo.engines(core, nxt)), len(topo.engines(prv, core))
+
+    def ts(out, in0, s1, s2, o0, o1, r, w=(), p=()):
+        args = (out, in0, s1, s2, o0) if o1 is None else (out, in0, s1, s2, o0, o1)
+        op("v", v.tensor_scalar, args, r, w, p)
+
+    def tt(out, a, b, o, r, w=(), p=()):
+        op("v", v.tensor_tensor, (out, a, b, o), r, w, p)
+
+    def cp(out, a, r, w=(), p=()):
+        op("v", v.tensor_copy, (out, a), r, w, p)
+
+    def scan(out, d0, d1, o0, o1, r, w):
+        op("v", v.tensor_tensor_scan, (out, d0, d1, 0.0, o0, o1), r, (w,))
+
+    def act(out, a, f, r, w=(), p=(), **kw):
+        op("s", sc.activation, (out, a, f), r, w, p, kw=kw)
+
+    def mm(out, l, rh, st, sp, r, w):
+        op("t", te.matmul, (out, l, rh, st, sp), r, (w,), acc=not st)
+
+    def fill(ap, x, w=(), p=()):
+        op("v", v.memset, (ap, x), (), w, p)
+
+    def iota(out, pat, base, ch, w, **kw):
+        op("g", g.iota, (out, pat, base, ch), (), (w,), kw=kw)
+    C = lambda j: T.col[:, j:j + 1]
+    M1, M0, SCT, BIT, CEN, DUMP, THR, OFF, CEN0 = range(9)
+    inC = lambda t: T.inC[:, 272 * t:272 * t + 256]
+    inP = lambda t: T.inC[:, 272 * t + 256:272 * t + 272]
+    outC = lambda t: T.outC[:, 272 * t:272 * t + 256]
+    outO = lambda t: T.outC[:, 272 * t + 256:272 * t + 272]
+    inW = lambda t: T.inW[:, 256 * t:256 * t + 256]
+    outW = lambda t: T.outW[:, 256 * t:256 * t + 256]
+    last16 = lambda b: b[:, 15::16]
+
+    dma("s", T.ci[:], T.cand[:], "cand", w=("ci",))
+    dma("y", inW(0), T.want[:], "want", w=("inW0",))
+    dma("y", T.featW[:, 0:W], T.feat[:], "f0", w=("feat",))
+    dma("s", T.mkb[:], T.mkey[:], "mkey", w=("mkb",))
+    dma("s", T.moi[:], T.mobj[:], "mobj", w=("moi",))
+    dma("s", T.wti[:], T.wts[:], "wts", w=("wti",))
+    dma("s", T.lai[:], T.last[:], "last", w=("lai",))
+    for q in range(4):
+        dma("y", T.kidi[:, 1024 * q:1024 * q + 1024], T.kids[:, 1024 * q:1024 * q + 1024], "k%d" % q, w=("kidi%d" % q,))
+    dma("y", T.featW[:, W:2 * W], T.feat[:], "fd", w=("featd",))
+
+    iota(T.i1[:], [[16, 8], [0, 16]], 15, -1, "i1")
+    iota(T.i2[:], [[0, 16], [1, 16]], 128, -1, "i2")
+    iota(T.i5[:], [[0, 8]], 0, 1, "i5")
+    iota(T.i3[:], [[0, 16], [1, 16]], 0, 1, "i3")
+    iota(T.i4[:], [[1, 16]], 0, 0, "i4")
+    iota(T.i6[:], [[0, 16], [4096, 16]], 2048, 0, "i6")
+    iota(T.idW[:], [[1, W + 16]], 0, 0, "idW", allow_small_or_imprecise_dtypes=True)
+    fill(T.LH[:], 0.0, w=("LH",))
+    ts(T.i1b[:], T.i1[:], 4, None, ALU.arith_shift_right, None, ("i1",), ("i1b",))
+    ts(T.i2b[:], T.i2[:], 15, None, ALU.bitwise_and, None, ("i2",), ("i2b",))
+    ts(T.ib[:, 0:1], T.i5[:, 0:1], 4, 1, ALU.logical_shift_right, ALU.bitwise_and, ("i5",), ("ib0",))
+    ts(T.ib[:, 1:2], T.i5[:, 0:1], 3, 1, ALU.logical_shift_right, ALU.bitwise_and, ("i5",), ("ib1",))
+    ts(T.ib[:, 2:3], T.i5[:, 0:1], 15, None, ALU.bitwise_and, None, ("i5",), ("ib2",))
+    ts(T.blk[:], T.i1b[:], 0.0, None, ALU.is_equal, None, ("i1b",), ("blk",))
+    ts(T.diag[:], T.i2b[:], 0.0, None, ALU.is_equal, None, ("i2b",), ("diag",))
+    cp(C(M1), T.ib[:, 0:1], ("ib0",), ("m1",))
+    ts(C(M0), T.ib[:, 0:1], -1.0, 1.0, ALU.mult, ALU.add, ("ib0",), ("m0",))
+    ts(C(SCT), T.ib[:, 1:2], -1.0, 1.0, ALU.mult, ALU.add, ("ib1",), ("sct",))
+    ts(C(DUMP), T.ib[:, 2:3], float(W), None, ALU.add, None, ("ib2",), ("dump",))
+    fill(C(CEN0), 2048.0, w=("cen0",))
+    fill(T.ones[:], 1.0, w=("ones",))
+    ts(T.b8[:], T.blk[:, 0::16], 65536.0, None, ALU.mult, None, ("blk",), ("b8",))
+    tt(T.If[:], T.blk[:], T.diag[:, 0:128], ALU.mult, ("blk", "diag"), ("If",))
+    ts(C(BIT), C(SCT), 4097.0, -1.0, ALU.mult, ALU.add, ("sct",), ("bit",))
+    ts(C(CEN), C(SCT), 4096.0, 2048.0, ALU.mult, ALU.add, ("sct",), ("cen",))
+    ts(C(OFF), C(SCT), 4096.0, None, ALU.mult, None, ("sct",), ("off",))
+    cp(T.expl[:], T.i4[:], ("i4",), ("expl",))
+    cp(T.I16[:], T.If[:], ("If",), ("I16",))
+    cp(T.IB[:], T.If[:], ("If",), ("IB",))
+    ts(T.IN[:], T.If[:], -1.0, None, ALU.mult, None, ("If",), ("IN",))
+    for b in range(16):
+        e = 129 * b + 113
+        act(T.LH[:, 129 * b:e:16], T.b8[:], AF.Copy, ("b8",), p=("LH",))
+    cp(T.Kc[:], T.i6[:], ("i6",), ("Kc",))
+    cp(T.inC[:, 0:256], T.ci[:], ("ci",), ("inC0",))
+    cp(T.R16[:, :, 0:16], T.I16[:], ("I16",), p=("R16",))
+    cp(T.R16[:, :, 16:32], T.I16[:], ("I16",), p=("R16",))
+
+    def expand(t):
+        for k in range(KD, 16):
+            act(T.Wx[:, k::16], inW(t), AF.Copy, ("inW%d" % t,), p=("Wx",))
+
+    def expand_v(t):
+        for k in range(KD):
+            cp(T.Wx[:, k::16], inW(t), ("inW%d" % t,), p=("Wx",))
+    expand(0)
+    expand_v(0)
+    for nm, x, y in (("RST", 0.0, BIG), ("RZ", BIG, 0.0), ("R1", 1.0, 0.0), ("R2", 2.0, 0.0)):
+        fill(T[nm][:], x, w=(nm,))
+        fill(T[nm][:, 0::16], y, p=(nm,))
+    scan(T.t3[:], T.R2[:], T.diag[:], ALU.mult, ALU.add, ("R2", "diag"), "t3")
+    ts(C(THR), T.t3[:, 15:16], 2.0, None, ALU.mult, None, ("t3",), ("thr",))
+    ts(T.offc[:], T.diag[:, 0:16], 0.0, C(OFF), ALU.mult, ALU.add, ("diag", "off"), ("offc",))
+    fill(T.limA[:], 65536.0 * (LIM - 1), w=("limA",))
+    fill(T.limB[:], 65536.0 * LIM, w=("limB",))
+    cp(T.wtf[:], T.wti[:], ("wti",), ("wtf",))
+    ts(T.wblk[:], T.blk[:], T.wtf[:], None, ALU.mult, None, ("blk", "wtf"), ("wblk",))
+    ts(T.i3b[:], T.i3[:], 15, None, ALU.bitwise_and, None, ("i3",), ("i3b",))
+    ts(T.t1[:], T.i3b[:], -16384.0, 262144.0 + 4096.0, ALU.mult, ALU.add, ("i3b",), ("t1",))
+    ts(T.t2[:], T.i3b[:], 10.0, 4096.0, ALU.is_lt, ALU.mult, ("i3b",), ("t2",))
+    ts(T.t3[:], T.i3b[:], 4.0, 4096.0, ALU.is_lt, ALU.mult, ("i3b",), ("t3",))
+    tt(T.t1[:], T.t1[:], T.t2[:], ALU.add, ("t1", "t2"), ("t1",))
+    tt(T.CJ[:], T.t1[:], T.t3[:], ALU.add, ("t1", "t3"), ("CJ",))
+    ts(T.CJ2[:], T.CJ[:], 2048.0, None, ALU.add, None, ("CJ",), ("CJ2",))
+    for b in range(16):
+        cp(T.SH[:, 128 * b:128 * b + 128], T.R16[:, :, b:b + 16], ("R16",), p=("SH",))
+
+    def flip(src, X, XT, nx, scl=None):
+        for h, m, nm in ((0, M0, "m0"), (1, M1, "m1")):
+            o = X[:, :, 16 * h:16 * h + 16]
+            if scl is None:
+                ts(o, src[0], C(m), None, ALU.mult, None, (src[1], nm), p=(nx,))
+            else:
+                ts(o, src[0], scl[0], C(m), scl[2], ALU.mult, (src[1], nm, scl[1]), p=(nx,))
+        op("v", v.transpose, (XT[:], X[:]), (nx,), (nx + "T",))
+    cp(T.mk16[:], T.mkb[:], ("mkb",), ("mk16",))
+    ts(T.mo16[:], T.moi[:], 2048.0, None, ALU.subtract, None, ("moi",), ("mo16",))
+    for b in range(16):
+        op("t", te.matmul, (T.pA[:, b:256:16], T.SH[:, 128 * b:128 * b + 128], T.mk16[:, b::16], True, True), ("SH", "mk16"), p=("pA",))
+    for b in range(16):
+        op("t", te.matmul, (T.pB[:, b:256:16], T.SH[:, 128 * b:128 * b + 128], T.mo16[:, b::16], True, True), ("SH", "mo16"), p=("pB",))
+    flip((T.pA[:, 0:256], "pA"), T.X, T.XT, "X")
+    flip((T.pB[:, 0:256], "pB"), T.Y, T.YT, "Y")
+
+    def halves(out, XT, nx, w):
+        mm(out, T.I16[:], XT[:, :, 0:16], True, False, ("I16", nx + "T"), w)
+        mm(out, T.I16[:], XT[:, :, 16:32], False, True, ("I16", nx + "T"), w)
+    halves(T.pA[:, 0:256], T.XT, "X", "pA")
+    halves(T.pB[:, 0:256], T.YT, "Y", "pB")
+    cp(T.MK[:], T.pA[:, 0:256], ("pA",), ("MK",))
+    tt(T.pM[:, 0:256], T.pB[:, 0:256], T.CJ2[:], ALU.add, ("pB", "CJ2"), ("pM",))
+    ts(T.LX[:, 0:16], T.lai[:], C(M0), None, ALU.mult, None, ("lai", "m0"), p=("LX",))
+    ts(T.LX[:, 16:32], T.lai[:], C(M1), None, ALU.mult, None, ("lai", "m1"), p=("LX",))
+    op("v", v.transpose, (T.LT[:], T.LX[:]), ("LX",), ("LT",))
+    tt(T.prev0[:], T.LT[:, 0:16], T.LT[:, 16:32], ALU.add, ("LT",), ("prev0",))
+
+    kbank = ["pA", "pB", "pC", "pW"]
+
+    def keymm(i):
+        p = kbank[i % 4]
+        mm(T[p][:], T.wblk[:], T.featW[:, 512 * i:512 * i + 512], True, True, ("wblk", "feat"), p)
+
+    def keyev(i):
+        p = kbank[i % 4]
+        act(T.keyW[:, 512 * i:512 * i + 512], T[p][:], AF.Copy, (p,), p=("keyW",))
+
+    def scatters():
+        for c in range(15, -1, -1):
+            tt(T.kid[:].indirect(T.s2u[:, 2 * c:2 * c + 1]), T.cf[:, 16 * c:16 * c + 16], T.offc[:], ALU.subtract, ("s2u", "cf", "offc"), ("kid",))
+
+    def limit():
+        mm(T.pC[:, 0:16], T.ones[:], T.cov[:], True, True, ("ones", "cov"), "pC")
+        op("v", v.tensor_reduce, (T.cs[:], T.pC[:, 0:16], AxisListType.X, ALU.add), ("pC",), ("cs",))
+        cp(T.csi[:], T.cs[:], ("cs",), ("csi",))
+        ts(T.csa[:], T.csi[:], 15, None, ALU.bitwise_and, None, ("csi",), ("csa",))
+        ts(T.limA[:], T.csa[:], 65536.0, 65536.0 * (LIM - 1), ALU.mult, ALU.add, ("csa",), ("limA",))
+        ts(T.limB[:], T.csa[:], 65536.0, 65536.0 * LIM, ALU.mult, ALU.add, ("csa",), ("limB",))
+
+    if True:
+        for i in range(4):
+            keymm(i)
+    for t in range(STEPS):
+        ic, iw = "inC%d" % t, "inW%d" % t
+        if t:
+            arrive("w%d" % t, nin, (iw,))
+            arrive("c%d" % t, nin, (ic,))
+            expand(t)
+            expand_v(t)
+        fw = 2 * W if t else W
+        mm(T.pv[:, 0:256], T.I16[:], T.Kc[:], True, False, ("I16", "Kc"), "pv")
+        mm(T.pL[:, 0:256], T.I16[:], T.Kc[:], True, False, ("I16", "Kc"), "pL")
+        for x, (c0, c1) in enumerate(CH):
+            tt(T.D[:, 256 * c0:256 * c1], T.featW[:, 0:fw].indirect(T.inC[:, 272 * t + 16 * c0:272 * t + 16 * c1]), T.Wx[:, 256 * c0:256 * c1], ALU.subtract,
+               ("feat", ic, "Wx") + (("featd",) if t else ()), ("D%d" % x,))
+            if x == 0:
+                ce = (C(CEN if t else CEN0), "cen" if t else "cen0", ALU.subtract)
+                flip((inC(t), ic), T.X, T.XT, "X", ce)
+            if t == 0:
+                keyev(x)
+                if x + 4 < 8:
+                    keymm(x + 4)
+            act(T.A[:, c0:c1, :], T.D[:, 256 * c0:256 * c1], AF.Abs, ("D%d" % x,), ("A%d" % x,))
+            if x == 2:
+                act(T.Lp[:], T.pL[:, 0:256], AF.Identity, ("pL", "limA"), ("Lp",), bias=T.limA[:])
+            for b in range(16):
+                mm(T.pv[:, 16 * c0:16 * c1], T.LH[:, 128 * b:128 * b + 128], T.A[:, c0:c1, 16 * b:16 * b + 16], False, x == len(CH) - 1 and b == 15,
+                   ("LH", "A%d" % x), "pv")
+            if x == 0:
+                for p, e in (("pv", False), ("pL", True)):
+                    mm(T[p][:, 0:256], T.I16[:], T.XT[:, :, 0:16], False, False, ("I16", "XT"), p)
+                    mm(T[p][:, 0:256], T.I16[:], T.XT[:, :, 16:32], False, e, ("I16", "XT"), p)
+        if t == 0:
+            for i in range(5, 8):
+                keyev(i)
+            for q in range(4):
+                cp(T.kid[:, 1024 * q:1024 * q + 1024], T.kidi[:, 1024 * q:1024 * q + 1024], ("kidi%d" % q,), p=("kid",))
+        else:
+            scatters()
+        tt(T.vm[:], T.pv[:, 0:256], T.Lp[:], ALU.max, ("pv", "Lp"), ("vm",))
+        scan(T.vI[:], T.RST[:], T.vm[:], ALU.max, ALU.min, ("RST", "vm"), "vI")
+        ts(T.oa[:], last16(T.vI), 4095, None, ALU.bitwise_and, None, ("vI",), ("oa",))
+        oc, oo = "outC%d" % t, "outO%d" % t
+        cp(outO(t), T.oa[:], ("oa",), (oo,))
+        if t < STEPS - 1:
+            act(T.xo[:], T.featW[:, 0:W].indirect(outO(t)), AF.Copy, ("feat", oo), ("xo",))
+            mm(T.pW[:, 0:256], T.IB[:], T.xo[:], True, False, ("IB", "xo"), "pW")
+            mm(T.pW[:, 0:256], T.IN[:], inW(t), False, True, ("IN", iw), "pW")
+            act(outW(t), T.pW[:, 0:256], AF.Abs, ("pW",), ("outW%d" % t,))
+            need("g", ("outW%d" % t,))
+            g.remote_dma(inW(t + 1), outW(t), T.sem["w%d" % (t + 1)], T.sem.ls, pid, rid, mask)
+            cnt["ls"] = cnt.get("ls", 0) + nout
+        tt(T.ky[:], T.keyW[:].indirect(outO(t)), T.diag[:], ALU.mult, ("keyW", oo, "diag"), ("ky",))
+        scan(T.ks[:], T.R1[:], T.ky[:], ALU.mult, ALU.add, ("R1", "ky"), "ks")
+        ts(T.key[:], last16(T.ks), 63, None, ALU.bitwise_and, None, ("ks",), ("key",))
+        tt(T.eq[:], T.key[:].indirect(T.expl[:]), T.MK[:], ALU.is_equal, ("key", "expl", "MK"), ("eq",))
+        tt(T.em[:], T.eq[:], T.pM[:, 0:256], ALU.mult, ("eq", "pM"), ("em",))
+        scan(T.es[:], T.RZ[:], T.em[:], ALU.min, ALU.max, ("RZ", "em"), "es")
+        ev = last16(T.es)
+        ts(T.eo[:], ev, 4095, None, ALU.bitwise_and, None, ("es",), ("eo",))
+        ts(T.sT[:], ev, 13, 1, ALU.logical_shift_right, ALU.bitwise_and, ("es",), ("sT",))
+        ts(T.sL[:], ev, 12, 1, ALU.logical_shift_right, ALU.bitwise_and, ("es",), ("sL",))
+        tt(T.de[:], T.eo[:], T.oa[:], ALU.subtract, ("eo", "oa"), ("de",))
+        tt(T.tT[:], T.sT[:], T.de[:], ALU.mult, ("sT", "de"), ("tT",))
+        tt(T.tL[:], T.sL[:], T.de[:], ALU.mult, ("sL", "de"), ("tL",))
+        tt(T.lT[:], T.tT[:], T.oa[:], ALU.add, ("tT", "oa"), ("lT",))
+        cp(T.uT[:], T.lT[:], ("lT",), ("uT",))
+        tt(T.lL[:], T.tL[:], T.oa[:], ALU.add, ("tL", "oa"), ("lL",))
+        cp(T.uL[:], T.lL[:], ("lL",), ("uL",))
+        act(T.top[:], T.kid[:, 0:W].indirect(T.uT[:]), AF.Identity, ("kid", "uT", "sct", "bit"), ("top",), bias=C(BIT), scale=C(SCT))
+        ts(T.ncd[:], ev, 1.0, C(DUMP), ALU.is_lt, ALU.mult, ("es", "dump"), ("ncd",))
+        ts(T.na[:], last16(T.vI), T.limB[:], None, ALU.is_ge, None, ("vI", "limB"), ("na",))
+        if t < STEPS - 1:
+            ts(T.cov[:], ev, 1.0, None, ALU.is_ge, None, ("es",), ("cov",))
+        tt(T.s1[:], T.oa[:], T.ncd[:], ALU.max, ("oa", "ncd"), ("s1",))
+        tt(T.cf[:], T.kid[:, 0:W].indirect(T.uL[:]), T.top[:], ALU.max, ("kid", "uL", "top"), ("cf",))
+        cp(outC(t), T.cf[:], ("cf",), (oc,))
+        wd = 272 if t < STEPS - 1 else 256
+        need("g", (oc, oo))
+        g.remote_dma(T.inC[:, 272 * t + 272:272 * t + 272 + wd], T.outC[:, 272 * t:272 * t + wd], T.sem["c%d" % (t + 1)], T.sem.ls, pid, rid, mask)
+        cnt["ls"] = cnt.get("ls", 0) + nout
+        cp(T.s1u[:], T.s1[:], ("s1",), ("s1u",))
+        act(T.gl[:], T.idW[:].indirect(T.s1u[:]), AF.Copy, ("idW", "s1u"), ("gl",))
+        q = 5 * t % 16
+        pr, prn = (inP(t), ic) if t else (T.prev0[:], "prev0")
+        tt(T.dk[:], T.key[:], T.MK[:, q::16], ALU.subtract, ("key", "MK"), ("dk",))
+        ts(T.pn[:], pr, T.CJ[:, q:q + 1], None, ALU.add, None, (prn, "CJ"), ("pn",))
+        tt(T.dk2[:], T.dk[:], T.na[:], ALU.mult, ("dk", "na"), ("dk2",))
+        tt(T.dn[:], T.pn[:], T.pM[:, q:256:16], ALU.subtract, ("pn", "pM"), ("dn",))
+        tt(T.MK[:, q::16], T.MK[:, q::16], T.dk2[:], ALU.add, ("dk2",), ("MK",))
+        tt(T.dn2[:], T.dn[:], T.na[:], ALU.mult, ("dn", "na"), ("dn2",))
+        tt(T.pM[:, q:256:16], T.dn2[:], T.pM[:, q:256:16], ALU.add, ("dn2",), ("pM",))
+        if t < STEPS - 1:
+            limit()
+        tt(T.eq2[:], T.s1[:].indirect(T.expl[:]), T.gl[:], ALU.is_equal, ("s1", "expl", "gl"), ("eq2",))
+        scan(T.dsum[:], T.R2[:], T.eq2[:], ALU.mult, ALU.add, ("R2", "eq2"), "dsum")
+        ts(T.dd[:], last16(T.dsum), C(THR), C(DUMP), ALU.is_ge, ALU.mult, ("dsum", "thr", "dump"), ("dd",))
+        tt(T.s2[:], T.s1[:], T.dd[:], ALU.max, ("s1", "dd"), ("s2",))
+        cp(T.s2u[:, 0::2], T.s2[:], ("s2",), ("s2u",))
+    scatters()
+    yb = ["pA", "pB", "pC", "pW"]
+    for i in range(1, 8):
+        p = yb[i % 4]
+        act(T[p][:], T.kid[:, 512 * i:512 * i + 512], AF.Copy, ("kid",), (p,), scale=float(i + 1))
+        if i == 1:
+            tt(T.t1[:], T.pM[:, 0:256], T.CJ2[:], ALU.subtract, ("pM", "CJ2"), ("t1",))
+            ts(T.t2[:], T.MK[:], 1.0 / 64, None, ALU.mult, None, ("MK",), ("t2",))
+            flip((T.t1[:], "t1"), T.X, T.XT, "X")
+            flip((T.t2[:], "t2"), T.Y, T.YT, "Y")
+            for b in range(16):
+                sh = T.SH[:, 128 * (-b % 16):128 * (-b % 16) + 128]
+                for e, (XT, nx, o) in enumerate(((T.XT, "XT", 0), (T.XT, "XT", 16), (T.YT, "YT", 0), (T.YT, "YT", 16))):
+                    op("t", te.matmul, (T.pv[:, b:256:16], sh, XT[:, :, o + b], e == 0, e == 3), ("SH", nx), p=("pv",))
+            arrive("c%d" % STEPS, nin, ("inC%d" % STEPS,))
+        tt(T.acc[:], T.kid[:, 0:512] if i == 1 else T.acc[:], T[p][:], ALU.add, ("kid" if i == 1 else "acc", p), ("acc",))
+        if i == 4:
+            ts(T.yno[:], inC(STEPS), C(OFF), None, ALU.subtract, None, ("inC%d" % STEPS, "off"), ("yno",))
+            dma("y", T.yn[:], T.yno[:], "yn", r=("yno",))
+    act(T.ymo[:], T.pv[:, 0:256], AF.Copy, ("pv",), ("ymo",), scale=64.0, bias=131072.0)
+    dma("y", T.yd[:], T.acc[:], "yd", r=("acc",))
+    dma("y", T.ymu[:], T.ymo[:], "ymu", r=("ymo",))
+    finish("g")

@@ -1,46 +1,50 @@
 from concourse.mybir import AluOpType as ALU, AxisListType, ActivationFunctionType as AF
 
 STEPS, W, L, LIM = 8, 4096, 256, 60
-CH = [(0, 4), (4, 8), (8, 12), (12, 14), (14, 16)]
-KD = 6
+CH = [(0, 2), (2, 6), (6, 10), (10, 14)]
+OWN = 14
+XF = 1
+KD, KG = 7, 3
 BIG = float(2 ** 26)
 
 _f, _b, _h, _i, _u = "float32", "bfloat16", "float16", "int32", "uint16"
 SCRATCH = {
     "featW": ("sbuf", [128, 2 * W], _b), "kidi": ("sbuf", [128, W], _i), "kid": ("sbuf", [128, W + 16], _f),
     "keyW": ("sbuf", [128, W], _f), "idW": ("sbuf", [128, W + 16], _f),
-    "Wx": ("sbuf", [128, W], _b), "D": ("sbuf", [128, W], _b), "A": ("sbuf", [128, 16, 256], _b),
+    "Wx": ("sbuf", [128, W], _b), "D": ("sbuf", [128, W], _b), "A": ("sbuf", [128, 16, 256], _b), "raw": ("sbuf", [128, 512], _b),
     "LH": ("sbuf", [128, 2048], _b), "SH": ("sbuf", [128, 2048], _h), "R16": ("sbuf", [128, 8, 32], _h),
-    "i1": ("sbuf", [128, 128], _i), "i1b": ("sbuf", [128, 128], _i), "i2": ("sbuf", [128, 256], _i), "i2b": ("sbuf", [128, 256], _i),
-    "i3": ("sbuf", [128, 256], _i), "i3b": ("sbuf", [128, 256], _i), "i4": ("sbuf", [128, 16], _i), "i5": ("sbuf", [128, 8], _i),
-    "i6": ("sbuf", [128, 256], _i), "ib": ("sbuf", [128, 8], _i),
+    "i1": ("sbuf", [128, 128], _i), "i1b": ("sbuf", [128, 128], _i), "i2": ("sbuf", [128, 16], _i), "i2b": ("sbuf", [128, 16], _i),
+    "i3": ("sbuf", [128, 16], _i), "i3b": ("sbuf", [128, 16], _i), "i4": ("sbuf", [128, 16], _i), "i5": ("sbuf", [128, 16], _i), "i6": ("sbuf", [128, 16], _i),
+    "bi": ("sbuf", [128, 16], _i), "exb": ("sbuf", [128, 16], _u), "dg": ("sbuf", [128, 16], _f), "ib": ("sbuf", [128, 8], _i),
+    "a1": ("sbuf", [128, 16], _f), "a2": ("sbuf", [128, 16], _f), "a3": ("sbuf", [128, 16], _f), "a4": ("sbuf", [128, 16], _f),
     "blk": ("sbuf", [128, 128], _f), "diag": ("sbuf", [128, 256], _f), "I16": ("sbuf", [128, 128], _h), "IB": ("sbuf", [128, 128], _b),
     "IN": ("sbuf", [128, 128], _b), "If": ("sbuf", [128, 128], _f), "ones": ("sbuf", [128, 128], _b), "wblk": ("sbuf", [128, 128], _b),
-    "b8": ("sbuf", [128, 8], _b), "Kc": ("sbuf", [128, 256], _h), "expl": ("sbuf", [128, 16], _u),
+    "b8": ("sbuf", [128, 8], _b), "Kc": ("sbuf", [128, 256], _b), "expl": ("sbuf", [128, 16], _u),
     "RST": ("sbuf", [128, 256], _f), "RZ": ("sbuf", [128, 256], _f), "R1": ("sbuf", [128, 256], _f), "R2": ("sbuf", [128, 256], _f),
-    "CJ": ("sbuf", [128, 256], _f), "CJ2": ("sbuf", [128, 256], _f), "t1": ("sbuf", [128, 256], _f), "t2": ("sbuf", [128, 256], _f), "t3": ("sbuf", [128, 256], _f),
+    "CJ": ("sbuf", [128, 16], _f), "CJ2": ("sbuf", [128, 256], _f), "t3": ("sbuf", [128, 256], _f),
     "col": ("sbuf", [128, 16], _f), "offc": ("sbuf", [128, 16], _f), "wti": ("sbuf", [128, 1], _i), "wtf": ("sbuf", [128, 1], _f),
     "ci": ("sbuf", [128, 256], _i), "mkb": ("sbuf", [128, 256], _b), "moi": ("sbuf", [128, 256], _i), "mk16": ("sbuf", [128, 256], _h), "mo16": ("sbuf", [128, 256], _h),
     "lai": ("sbuf", [128, 16], _i), "LX": ("sbuf", [128, 32], _f), "LT": ("sbuf", [128, 32], _f), "prev0": ("sbuf", [128, 16], _f),
     "X": ("sbuf", [128, 16, 32], _h), "XT": ("sbuf", [128, 16, 32], _h), "Y": ("sbuf", [128, 16, 32], _h), "YT": ("sbuf", [128, 16, 32], _h),
     "MK": ("sbuf", [128, 256], _f), "Lp": ("sbuf", [128, 256], _f), "vm": ("sbuf", [128, 256], _f), "vI": ("sbuf", [128, 256], _i),
-    "oa": ("sbuf", [128, 16], _i), "ky": ("sbuf", [128, 256], _f), "ks": ("sbuf", [128, 256], _i), "key": ("sbuf", [128, 16], _i),
+    "oa": ("sbuf", [128, 16], _i), "kk": ("sbuf", [128, 16], _i), "po": ("sbuf", [128, 16], _i), "pb": ("sbuf", [128, 16], _i), "pbb": ("sbuf", [128, 16], _i), "pu": ("sbuf", [128, 16], _u),
+    "ky": ("sbuf", [128, 256], _f), "ks": ("sbuf", [128, 256], _i), "key": ("sbuf", [128, 16], _i),
     "eq": ("sbuf", [128, 256], _f), "em": ("sbuf", [128, 256], _f), "es": ("sbuf", [128, 256], _i),
     "eo": ("sbuf", [128, 16], _i), "sT": ("sbuf", [128, 16], _i), "sL": ("sbuf", [128, 16], _i), "de": ("sbuf", [128, 16], _i),
-    "tT": ("sbuf", [128, 16], _i), "tL": ("sbuf", [128, 16], _i), "lT": ("sbuf", [128, 16], _i), "lL": ("sbuf", [128, 16], _i),
-    "uT": ("sbuf", [128, 16], _u), "uL": ("sbuf", [128, 16], _u), "top": ("sbuf", [128, 256], _f), "cf": ("sbuf", [128, 256], _f),
+    "tT": ("sbuf", [128, 16], _i), "tL": ("sbuf", [128, 16], _i), "l2": ("sbuf", [128, 32], _i), "u2": ("sbuf", [128, 32], _u),
+    "top": ("sbuf", [128, 256], _f), "cf": ("sbuf", [128, 256], _f),
     "na": ("sbuf", [128, 16], _f), "cov": ("sbuf", [128, 16], _b), "ncd": ("sbuf", [128, 16], _f), "s1": ("sbuf", [128, 16], _f), "s1u": ("sbuf", [128, 16], _u),
     "gl": ("sbuf", [128, 256], _f), "eq2": ("sbuf", [128, 256], _f), "dsum": ("sbuf", [128, 256], _f), "dd": ("sbuf", [128, 16], _f), "s2": ("sbuf", [128, 16], _f), "s2u": ("sbuf", [128, 32], _u),
     "dk": ("sbuf", [128, 16], _f), "dk2": ("sbuf", [128, 16], _f), "pn": ("sbuf", [128, 16], _f), "dn": ("sbuf", [128, 16], _f), "dn2": ("sbuf", [128, 16], _f),
-    "cs": ("sbuf", [128, 1], _f), "csi": ("sbuf", [128, 1], _i), "csa": ("sbuf", [128, 1], _i), "limA": ("sbuf", [128, 1], _f), "limB": ("sbuf", [128, 1], _f),
-    "xo": ("sbuf", [128, 256], _b), "yno": ("sbuf", [128, 256], _f), "ymo": ("sbuf", [128, 256], _f), "acc": ("sbuf", [128, 512], _f),
+    "cs": ("sbuf", [128, 1], _f), "csi": ("sbuf", [128, 1], _i), "csa": ("sbuf", [128, 1], _i), "limA": ("sbuf", [128, 1], _f),
+    "yno": ("sbuf", [128, 256], _f), "ymo": ("sbuf", [128, 256], _f), "acc": ("sbuf", [128, 512], _f),
     "outC": ("sbuf", [128, STEPS * 272], _u), "inC": ("sbuf", [128, (STEPS + 1) * 272], _u),
     "outW": ("sbuf", [128, STEPS * 256], _b), "inW": ("sbuf", [128, STEPS * 256], _b),
     "pv": ("psum", [128, 512], _f), "pL": ("psum", [128, 512], _f), "pM": ("psum", [128, 512], _f), "pC": ("psum", [128, 512], _f),
-    "pW": ("psum", [128, 512], _f), "pA": ("psum", [128, 512], _f), "pB": ("psum", [128, 512], _f),
+    "pW": ("psum", [128, 512], _f), "pA": ("psum", [128, 512], _f), "pB": ("psum", [128, 512], _f), "pX": ("psum", [128, 512], _f),
 }
 DMAS = ["cand", "want", "wts", "last", "mkey", "mobj", "f0", "fd", "k0", "k1", "k2", "k3", "yn", "ymu", "yd"]
-SEMAPHORES = ["sv", "st", "ss", "sg", "ls"] + ["d_" + n for n in DMAS] + ["w%d" % t for t in range(1, STEPS)] + ["c%d" % t for t in range(1, STEPS + 1)]
+SEMAPHORES = ["sv", "st", "ss", "sg", "ls"] + ["d_" + n for n in DMAS] + ["w%d" % t for t in range(1, STEPS)] + [x + "%d" % t for t in range(1, STEPS + 1) for x in "ab"]
 
 
 def make(g, T):
@@ -155,6 +159,11 @@ def rank_program(g, core, T, topo):
     def mm(out, l, rh, st, sp, r, w):
         op("t", te.matmul, (out, l, rh, st, sp), r, (w,), acc=not st)
 
+    def send(out, in_, sem, r):
+        need("g", r)
+        g.remote_dma(out, in_, T.sem[sem], T.sem.ls, pid, rid, mask)
+        cnt["ls"] = cnt.get("ls", 0) + nout
+
     def fill(ap, x, w=(), p=()):
         op("v", v.memset, (ap, x), (), w, p)
 
@@ -164,7 +173,6 @@ def rank_program(g, core, T, topo):
     M1, M0, SCT, BIT, CEN, DUMP, THR, OFF, CEN0 = range(9)
     inC = lambda t: T.inC[:, 272 * t:272 * t + 256]
     inP = lambda t: T.inC[:, 272 * t + 256:272 * t + 272]
-    outC = lambda t: T.outC[:, 272 * t:272 * t + 256]
     outO = lambda t: T.outC[:, 272 * t + 256:272 * t + 272]
     inW = lambda t: T.inW[:, 256 * t:256 * t + 256]
     outW = lambda t: T.outW[:, 256 * t:256 * t + 256]
@@ -181,160 +189,168 @@ def rank_program(g, core, T, topo):
         dma("y", T.kidi[:, 1024 * q:1024 * q + 1024], T.kids[:, 1024 * q:1024 * q + 1024], "k%d" % q, w=("kidi%d" % q,))
     dma("y", T.featW[:, W:2 * W], T.feat[:], "fd", w=("featd",))
 
+    iota(T.i5[:], [[0, 16]], 0, 1, "i5")
+    iota(T.i2[:], [[1, 16]], 128, -1, "i2")
     iota(T.i1[:], [[16, 8], [0, 16]], 15, -1, "i1")
-    iota(T.i2[:], [[0, 16], [1, 16]], 128, -1, "i2")
-    iota(T.i5[:], [[0, 8]], 0, 1, "i5")
-    iota(T.i3[:], [[0, 16], [1, 16]], 0, 1, "i3")
     iota(T.i4[:], [[1, 16]], 0, 0, "i4")
-    iota(T.i6[:], [[0, 16], [4096, 16]], 2048, 0, "i6")
+    iota(T.i3[:], [[1, 16]], 0, 1, "i3")
+    iota(T.i6[:], [[256, 16]], 0, 0, "i6")
+    iota(T.Kc[:], [[0, 16], [4096, 16]], 2048, 0, "Kc", allow_small_or_imprecise_dtypes=True)
     iota(T.idW[:], [[1, W + 16]], 0, 0, "idW", allow_small_or_imprecise_dtypes=True)
     fill(T.LH[:], 0.0, w=("LH",))
-    ts(T.i1b[:], T.i1[:], 4, None, ALU.arith_shift_right, None, ("i1",), ("i1b",))
     ts(T.i2b[:], T.i2[:], 15, None, ALU.bitwise_and, None, ("i2",), ("i2b",))
+    ts(T.bi[:], T.i5[:], 15, None, ALU.bitwise_and, None, ("i5",), ("bi",))
+    ts(T.i1b[:], T.i1[:], 4, None, ALU.arith_shift_right, None, ("i1",), ("i1b",))
     ts(T.ib[:, 0:1], T.i5[:, 0:1], 4, 1, ALU.logical_shift_right, ALU.bitwise_and, ("i5",), ("ib0",))
     ts(T.ib[:, 1:2], T.i5[:, 0:1], 3, 1, ALU.logical_shift_right, ALU.bitwise_and, ("i5",), ("ib1",))
-    ts(T.ib[:, 2:3], T.i5[:, 0:1], 15, None, ALU.bitwise_and, None, ("i5",), ("ib2",))
+    ts(T.dg[:], T.i2b[:], 0.0, None, ALU.is_equal, None, ("i2b",), ("dg",))
+    cp(T.exb[:], T.bi[:], ("bi",), ("exb",))
     ts(T.blk[:], T.i1b[:], 0.0, None, ALU.is_equal, None, ("i1b",), ("blk",))
-    ts(T.diag[:], T.i2b[:], 0.0, None, ALU.is_equal, None, ("i2b",), ("diag",))
+    act(T.diag[:], T.dg[:].indirect(T.exb[:]), AF.Copy, ("dg", "exb"), ("diag",))
+    ts(T.b8[:], T.blk[:, 0::16], 65536.0, None, ALU.mult, None, ("blk",), ("b8",))
     cp(C(M1), T.ib[:, 0:1], ("ib0",), ("m1",))
     ts(C(M0), T.ib[:, 0:1], -1.0, 1.0, ALU.mult, ALU.add, ("ib0",), ("m0",))
     ts(C(SCT), T.ib[:, 1:2], -1.0, 1.0, ALU.mult, ALU.add, ("ib1",), ("sct",))
-    ts(C(DUMP), T.ib[:, 2:3], float(W), None, ALU.add, None, ("ib2",), ("dump",))
+    ts(C(DUMP), T.bi[:, 0:1], float(W), None, ALU.add, None, ("bi",), ("dump",))
     fill(C(CEN0), 2048.0, w=("cen0",))
-    fill(T.ones[:], 1.0, w=("ones",))
-    ts(T.b8[:], T.blk[:, 0::16], 65536.0, None, ALU.mult, None, ("blk",), ("b8",))
+    for b in range(16):
+        act(T.LH[:, 129 * b:129 * b + 113:16], T.b8[:], AF.Copy, ("b8",), p=("LH",))
     tt(T.If[:], T.blk[:], T.diag[:, 0:128], ALU.mult, ("blk", "diag"), ("If",))
+    cp(T.inC[:, 0:256], T.ci[:], ("ci",), ("inCa0", "inCb0"))
+    cp(T.I16[:], T.If[:], ("If",), ("I16",))
+    cp(T.IB[:], T.If[:], ("If",), ("IB",))
+    ts(T.IN[:], T.If[:], -1.0, None, ALU.mult, None, ("If",), ("IN",))
+
+    def expand(t, q, k):
+        out, nm = T.Wx[:, k::16], "inW%d" % t
+        if q == "v":
+            cp(out, inW(t), (nm,), p=("Wx",))
+        elif q == "s":
+            act(out, inW(t), AF.Copy, (nm,), p=("Wx",))
+        else:
+            op("g", g.affine_select, (out, inW(t), [[0, 256]], ALU.is_equal, 0.0, 0, 0), (nm,), p=("Wx",))
+    for k in range(16):
+        expand(0, "v" if k < KD else "s", k)
+    cp(T.wtf[:], T.wti[:], ("wti",), ("wtf",))
+    ts(T.wblk[:], T.blk[:], T.wtf[:], None, ALU.mult, None, ("blk", "wtf"), ("wblk",))
+    fill(T.R1[:], 1.0, w=("R1",))
+    fill(T.R1[:, 0::16], 0.0, p=("R1",))
+    act(T.R2[:], T.R1[:], AF.Copy, ("R1",), ("R2",), scale=2.0)
+    act(T.RZ[:], T.R1[:], AF.Copy, ("R1",), ("RZ",), scale=BIG)
+    act(T.RST[:], T.R1[:], AF.Copy, ("R1",), ("RST",), scale=-BIG, bias=BIG)
     ts(C(BIT), C(SCT), 4097.0, -1.0, ALU.mult, ALU.add, ("sct",), ("bit",))
     ts(C(CEN), C(SCT), 4096.0, 2048.0, ALU.mult, ALU.add, ("sct",), ("cen",))
     ts(C(OFF), C(SCT), 4096.0, None, ALU.mult, None, ("sct",), ("off",))
     cp(T.expl[:], T.i4[:], ("i4",), ("expl",))
-    cp(T.I16[:], T.If[:], ("If",), ("I16",))
-    cp(T.IB[:], T.If[:], ("If",), ("IB",))
-    ts(T.IN[:], T.If[:], -1.0, None, ALU.mult, None, ("If",), ("IN",))
-    for b in range(16):
-        e = 129 * b + 113
-        act(T.LH[:, 129 * b:e:16], T.b8[:], AF.Copy, ("b8",), p=("LH",))
-    cp(T.Kc[:], T.i6[:], ("i6",), ("Kc",))
-    cp(T.inC[:, 0:256], T.ci[:], ("ci",), ("inC0",))
+    fill(T.limA[:], 65536.0 * (LIM - 1), w=("limA",))
+    ts(T.pbb[:], T.bi[:], 16.0, None, ALU.mult, None, ("bi",), ("pbb",))
+    ts(T.i3b[:], T.i3[:], 15, None, ALU.bitwise_and, None, ("i3",), ("i3b",))
+    tt(T.pb[:], T.pbb[:], T.i6[:], ALU.add, ("pbb", "i6"), ("pb",))
+    ts(T.a1[:], T.i3b[:], -16384.0, 262144.0 + 4096.0, ALU.mult, ALU.add, ("i3b",), ("a1",))
+    ts(T.a2[:], T.i3b[:], 10.0, 4096.0, ALU.is_lt, ALU.mult, ("i3b",), ("a2",))
+    ts(T.a3[:], T.i3b[:], 4.0, 4096.0, ALU.is_lt, ALU.mult, ("i3b",), ("a3",))
+    tt(T.a4[:], T.a1[:], T.a2[:], ALU.add, ("a1", "a2"), ("a4",))
+    tt(T.CJ[:], T.a4[:], T.a3[:], ALU.add, ("a4", "a3"), ("CJ",))
+    act(T.CJ2[:], T.CJ[:].indirect(T.exb[:]), AF.Copy, ("CJ", "exb"), ("CJ2",), bias=2048.0)
     cp(T.R16[:, :, 0:16], T.I16[:], ("I16",), p=("R16",))
     cp(T.R16[:, :, 16:32], T.I16[:], ("I16",), p=("R16",))
-
-    def expand(t):
-        for k in range(KD, 16):
-            act(T.Wx[:, k::16], inW(t), AF.Copy, ("inW%d" % t,), p=("Wx",))
-
-    def expand_v(t):
-        for k in range(KD):
-            cp(T.Wx[:, k::16], inW(t), ("inW%d" % t,), p=("Wx",))
-    expand(0)
-    expand_v(0)
-    for nm, x, y in (("RST", 0.0, BIG), ("RZ", BIG, 0.0), ("R1", 1.0, 0.0), ("R2", 2.0, 0.0)):
-        fill(T[nm][:], x, w=(nm,))
-        fill(T[nm][:, 0::16], y, p=(nm,))
-    scan(T.t3[:], T.R2[:], T.diag[:], ALU.mult, ALU.add, ("R2", "diag"), "t3")
-    ts(C(THR), T.t3[:, 15:16], 2.0, None, ALU.mult, None, ("t3",), ("thr",))
-    ts(T.offc[:], T.diag[:, 0:16], 0.0, C(OFF), ALU.mult, ALU.add, ("diag", "off"), ("offc",))
-    fill(T.limA[:], 65536.0 * (LIM - 1), w=("limA",))
-    fill(T.limB[:], 65536.0 * LIM, w=("limB",))
-    cp(T.wtf[:], T.wti[:], ("wti",), ("wtf",))
-    ts(T.wblk[:], T.blk[:], T.wtf[:], None, ALU.mult, None, ("blk", "wtf"), ("wblk",))
-    ts(T.i3b[:], T.i3[:], 15, None, ALU.bitwise_and, None, ("i3",), ("i3b",))
-    ts(T.t1[:], T.i3b[:], -16384.0, 262144.0 + 4096.0, ALU.mult, ALU.add, ("i3b",), ("t1",))
-    ts(T.t2[:], T.i3b[:], 10.0, 4096.0, ALU.is_lt, ALU.mult, ("i3b",), ("t2",))
-    ts(T.t3[:], T.i3b[:], 4.0, 4096.0, ALU.is_lt, ALU.mult, ("i3b",), ("t3",))
-    tt(T.t1[:], T.t1[:], T.t2[:], ALU.add, ("t1", "t2"), ("t1",))
-    tt(T.CJ[:], T.t1[:], T.t3[:], ALU.add, ("t1", "t3"), ("CJ",))
-    ts(T.CJ2[:], T.CJ[:], 2048.0, None, ALU.add, None, ("CJ",), ("CJ2",))
     for b in range(16):
         cp(T.SH[:, 128 * b:128 * b + 128], T.R16[:, :, b:b + 16], ("R16",), p=("SH",))
 
-    def flip(src, X, XT, nx, scl=None):
+    def flip(src, X, XT, nx, cen=None):
         for h, m, nm in ((0, M0, "m0"), (1, M1, "m1")):
             o = X[:, :, 16 * h:16 * h + 16]
-            if scl is None:
-                ts(o, src[0], C(m), None, ALU.mult, None, (src[1], nm), p=(nx,))
+            if cen is None:
+                ts(o, src[0], C(m), None, ALU.mult, None, src[1] + (nm,), p=(nx,))
             else:
-                ts(o, src[0], scl[0], C(m), scl[2], ALU.mult, (src[1], nm, scl[1]), p=(nx,))
+                ts(o, src[0], cen[0], C(m), ALU.subtract, ALU.mult, src[1] + (nm, cen[1]), p=(nx,))
         op("v", v.transpose, (XT[:], X[:]), (nx,), (nx + "T",))
-    cp(T.mk16[:], T.mkb[:], ("mkb",), ("mk16",))
-    ts(T.mo16[:], T.moi[:], 2048.0, None, ALU.subtract, None, ("moi",), ("mo16",))
-    for b in range(16):
-        op("t", te.matmul, (T.pA[:, b:256:16], T.SH[:, 128 * b:128 * b + 128], T.mk16[:, b::16], True, True), ("SH", "mk16"), p=("pA",))
-    for b in range(16):
-        op("t", te.matmul, (T.pB[:, b:256:16], T.SH[:, 128 * b:128 * b + 128], T.mo16[:, b::16], True, True), ("SH", "mo16"), p=("pB",))
-    flip((T.pA[:, 0:256], "pA"), T.X, T.XT, "X")
-    flip((T.pB[:, 0:256], "pB"), T.Y, T.YT, "Y")
 
     def halves(out, XT, nx, w):
         mm(out, T.I16[:], XT[:, :, 0:16], True, False, ("I16", nx + "T"), w)
         mm(out, T.I16[:], XT[:, :, 16:32], False, True, ("I16", nx + "T"), w)
+    cp(T.mk16[:], T.mkb[:], ("mkb",), ("mk16",))
+    ts(T.mo16[:], T.moi[:], 2048.0, None, ALU.subtract, None, ("moi",), ("mo16",))
+    for ps, src in (("pA", "mk16"), ("pB", "mo16")):
+        for b in range(16):
+            op("t", te.matmul, (T[ps][:, b:256:16], T.SH[:, 128 * b:128 * b + 128], T[src][:, b::16], True, True), ("SH", src), p=(ps,))
+    flip((T.pA[:, 0:256], ("pA",)), T.X, T.XT, "X")
+    flip((T.pB[:, 0:256], ("pB",)), T.Y, T.YT, "Y")
     halves(T.pA[:, 0:256], T.XT, "X", "pA")
     halves(T.pB[:, 0:256], T.YT, "Y", "pB")
-    cp(T.MK[:], T.pA[:, 0:256], ("pA",), ("MK",))
-    tt(T.pM[:, 0:256], T.pB[:, 0:256], T.CJ2[:], ALU.add, ("pB", "CJ2"), ("pM",))
     ts(T.LX[:, 0:16], T.lai[:], C(M0), None, ALU.mult, None, ("lai", "m0"), p=("LX",))
     ts(T.LX[:, 16:32], T.lai[:], C(M1), None, ALU.mult, None, ("lai", "m1"), p=("LX",))
     op("v", v.transpose, (T.LT[:], T.LX[:]), ("LX",), ("LT",))
     tt(T.prev0[:], T.LT[:, 0:16], T.LT[:, 16:32], ALU.add, ("LT",), ("prev0",))
+    scan(T.t3[:], T.R2[:], T.diag[:], ALU.mult, ALU.add, ("R2", "diag"), "t3")
+    ts(C(THR), T.t3[:, 15:16], 2.0, None, ALU.mult, None, ("t3",), ("thr",))
+    ts(T.offc[:], T.dg[:], 0.0, C(OFF), ALU.mult, ALU.add, ("dg", "off"), ("offc",))
+    act(T.MK[:], T.pA[:, 0:256], AF.Copy, ("pA",), ("MK",))
+    tt(T.pM[:, 0:256], T.pB[:, 0:256], T.CJ2[:], ALU.add, ("pB", "CJ2"), ("pM",))
+    fill(T.ones[:], 1.0, w=("ones",))
 
-    kbank = ["pA", "pB", "pC", "pW"]
+    kbank = ["pC", "pW", "pA", "pB"]
 
-    def keymm(i):
-        p = kbank[i % 4]
-        mm(T[p][:], T.wblk[:], T.featW[:, 512 * i:512 * i + 512], True, True, ("wblk", "feat"), p)
-
-    def keyev(i):
-        p = kbank[i % 4]
-        act(T.keyW[:, 512 * i:512 * i + 512], T[p][:], AF.Copy, (p,), p=("keyW",))
+    def keys(i0):
+        for i in range(i0, i0 + 4):
+            p = kbank[i % 4]
+            mm(T[p][:], T.wblk[:], T.featW[:, 512 * i:512 * i + 512], True, True, ("wblk", "feat"), p)
+        for i in range(i0, i0 + 4):
+            p = kbank[i % 4]
+            act(T.keyW[:, 512 * i:512 * i + 512], T[p][:], AF.Copy, (p,), p=("keyW",))
 
     def scatters():
         for c in range(15, -1, -1):
-            tt(T.kid[:].indirect(T.s2u[:, 2 * c:2 * c + 1]), T.cf[:, 16 * c:16 * c + 16], T.offc[:], ALU.subtract, ("s2u", "cf", "offc"), ("kid",))
+            tt(T.kid[:].indirect(T.s2u[:, 2 * c:2 * c + 1]), T.cf[:, 16 * c:16 * c + 16], T.offc[:], ALU.subtract, ("s2u", "cf0", "cf1", "offc"), ("kid",))
 
     def limit():
         mm(T.pC[:, 0:16], T.ones[:], T.cov[:], True, True, ("ones", "cov"), "pC")
-        op("v", v.tensor_reduce, (T.cs[:], T.pC[:, 0:16], AxisListType.X, ALU.add), ("pC",), ("cs",))
-        cp(T.csi[:], T.cs[:], ("cs",), ("csi",))
-        ts(T.csa[:], T.csi[:], 15, None, ALU.bitwise_and, None, ("csi",), ("csa",))
-        ts(T.limA[:], T.csa[:], 65536.0, 65536.0 * (LIM - 1), ALU.mult, ALU.add, ("csa",), ("limA",))
-        ts(T.limB[:], T.csa[:], 65536.0, 65536.0 * LIM, ALU.mult, ALU.add, ("csa",), ("limB",))
+        return [lambda: op("v", v.tensor_reduce, (T.cs[:], T.pC[:, 0:16], AxisListType.X, ALU.add), ("pC",), ("cs",)),
+                lambda: cp(T.csi[:], T.cs[:], ("cs",), ("csi",)),
+                lambda: ts(T.csa[:], T.csi[:], 15, None, ALU.bitwise_and, None, ("csi",), ("csa",)),
+                lambda: ts(T.limA[:], T.csa[:], 65536.0, 65536.0 * (LIM - 1), ALU.mult, ALU.add, ("csa",), ("limA",))]
 
-    if True:
-        for i in range(4):
-            keymm(i)
+    def dist(c0, c1, nm, stop):
+        for b in range(16):
+            mm(T.pv[:, 16 * c0:16 * c1], T.LH[:, 128 * b:128 * b + 128], T.A[:, c0:c1, 16 * b:16 * b + 16], False, stop and b == 15, ("LH", nm), "pv")
+    keys(0)
     for t in range(STEPS):
-        ic, iw = "inC%d" % t, "inW%d" % t
+        iw, ia, ibn, final = "inW%d" % t, "inCa%d" % t, "inCb%d" % t, t == STEPS - 1
         if t:
             arrive("w%d" % t, nin, (iw,))
-            arrive("c%d" % t, nin, (ic,))
-            expand(t)
-            expand_v(t)
+            arrive("a%d" % t, nin, (ia,))
+            arrive("b%d" % t, nin, (ibn,))
+            for k in range(16):
+                expand(t, "v" if k < KD else "s" if k < 16 - KG else "g", k)
         fw = 2 * W if t else W
-        mm(T.pv[:, 0:256], T.I16[:], T.Kc[:], True, False, ("I16", "Kc"), "pv")
-        mm(T.pL[:, 0:256], T.I16[:], T.Kc[:], True, False, ("I16", "Kc"), "pL")
+        fr = ("feat", "featd") if t else ("feat",)
+        mm(T.pv[:, 0:256], T.IB[:], T.Kc[:], True, False, ("IB", "Kc"), "pv")
+        mm(T.pL[:, 0:256], T.IB[:], T.Kc[:], True, False, ("IB", "Kc"), "pL")
         for x, (c0, c1) in enumerate(CH):
             tt(T.D[:, 256 * c0:256 * c1], T.featW[:, 0:fw].indirect(T.inC[:, 272 * t + 16 * c0:272 * t + 16 * c1]), T.Wx[:, 256 * c0:256 * c1], ALU.subtract,
-               ("feat", ic, "Wx") + (("featd",) if t else ()), ("D%d" % x,))
+               fr + ("Wx", ia) + ((ibn,) if c1 > 8 else ()), ("D%d" % x,))
+            if x == XF:
+                flip((inC(t), (ia, ibn)), T.X, T.XT, "X", (C(CEN if t else CEN0), "cen" if t else "cen0"))
             if x == 0:
-                ce = (C(CEN if t else CEN0), "cen" if t else "cen0", ALU.subtract)
-                flip((inC(t), ic), T.X, T.XT, "X", ce)
-            if t == 0:
-                keyev(x)
-                if x + 4 < 8:
-                    keymm(x + 4)
+                act(T.raw[:], T.featW[:, 0:fw].indirect(T.inC[:, 272 * t + 16 * OWN:272 * t + 256]), AF.Copy, fr + (ibn,), ("raw",))
+                mm(T.pX[:], T.IB[:], T.raw[:], True, False, ("IB", "raw"), "pX")
+                mm(T.pX[:], T.IN[:], T.Wx[:, 256 * OWN:4096], False, True, ("IN", "Wx"), "pX")
             act(T.A[:, c0:c1, :], T.D[:, 256 * c0:256 * c1], AF.Abs, ("D%d" % x,), ("A%d" % x,))
+            if x == 1:
+                act(T.A[:, OWN:16, :], T.pX[:], AF.Abs, ("pX",), ("A9",))
             if x == 2:
                 act(T.Lp[:], T.pL[:, 0:256], AF.Identity, ("pL", "limA"), ("Lp",), bias=T.limA[:])
-            for b in range(16):
-                mm(T.pv[:, 16 * c0:16 * c1], T.LH[:, 128 * b:128 * b + 128], T.A[:, c0:c1, 16 * b:16 * b + 16], False, x == len(CH) - 1 and b == 15,
-                   ("LH", "A%d" % x), "pv")
-            if x == 0:
-                for p, e in (("pv", False), ("pL", True)):
+            if x == len(CH) - 1 and not final:
+                act(T.D[:, 256 * OWN:4096], T.pX[:], AF.Abs, ("pX",), ("D9",))
+            if x == XF:
+                for p, e in (("pL", True), ("pv", False)):
                     mm(T[p][:, 0:256], T.I16[:], T.XT[:, :, 0:16], False, False, ("I16", "XT"), p)
                     mm(T[p][:, 0:256], T.I16[:], T.XT[:, :, 16:32], False, e, ("I16", "XT"), p)
+            dist(c0, c1, "A%d" % x, x == len(CH) - 1)
+            if x == 1:
+                dist(OWN, 16, "A9", False)
         if t == 0:
-            for i in range(5, 8):
-                keyev(i)
+            keys(4)
             for q in range(4):
                 cp(T.kid[:, 1024 * q:1024 * q + 1024], T.kidi[:, 1024 * q:1024 * q + 1024], ("kidi%d" % q,), p=("kid",))
         else:
@@ -342,16 +358,15 @@ def rank_program(g, core, T, topo):
         tt(T.vm[:], T.pv[:, 0:256], T.Lp[:], ALU.max, ("pv", "Lp"), ("vm",))
         scan(T.vI[:], T.RST[:], T.vm[:], ALU.max, ALU.min, ("RST", "vm"), "vI")
         ts(T.oa[:], last16(T.vI), 4095, None, ALU.bitwise_and, None, ("vI",), ("oa",))
-        oc, oo = "outC%d" % t, "outO%d" % t
+        oo = "outO%d" % t
+        if not final:
+            ts(T.kk[:], last16(T.vI), 12, 15, ALU.logical_shift_right, ALU.bitwise_and, ("vI",), ("kk",))
         cp(outO(t), T.oa[:], ("oa",), (oo,))
-        if t < STEPS - 1:
-            act(T.xo[:], T.featW[:, 0:W].indirect(outO(t)), AF.Copy, ("feat", oo), ("xo",))
-            mm(T.pW[:, 0:256], T.IB[:], T.xo[:], True, False, ("IB", "xo"), "pW")
-            mm(T.pW[:, 0:256], T.IN[:], inW(t), False, True, ("IN", iw), "pW")
-            act(outW(t), T.pW[:, 0:256], AF.Abs, ("pW",), ("outW%d" % t,))
-            need("g", ("outW%d" % t,))
-            g.remote_dma(inW(t + 1), outW(t), T.sem["w%d" % (t + 1)], T.sem.ls, pid, rid, mask)
-            cnt["ls"] = cnt.get("ls", 0) + nout
+        if not final:
+            tt(T.po[:], T.kk[:], T.pb[:], ALU.add, ("kk", "pb"), ("po",))
+            cp(T.pu[:], T.po[:], ("po",), ("pu",))
+            act(outW(t), T.D[:].indirect(T.pu[:]), AF.Abs, tuple("D%d" % x for x in range(len(CH))) + ("D9", "pu"), ("outW%d" % t,))
+            send(inW(t + 1), outW(t), "w%d" % (t + 1), ("outW%d" % t,))
         tt(T.ky[:], T.keyW[:].indirect(outO(t)), T.diag[:], ALU.mult, ("keyW", oo, "diag"), ("ky",))
         scan(T.ks[:], T.R1[:], T.ky[:], ALU.mult, ALU.add, ("R1", "ky"), "ks")
         ts(T.key[:], last16(T.ks), 63, None, ALU.bitwise_and, None, ("ks",), ("key",))
@@ -365,26 +380,27 @@ def rank_program(g, core, T, topo):
         tt(T.de[:], T.eo[:], T.oa[:], ALU.subtract, ("eo", "oa"), ("de",))
         tt(T.tT[:], T.sT[:], T.de[:], ALU.mult, ("sT", "de"), ("tT",))
         tt(T.tL[:], T.sL[:], T.de[:], ALU.mult, ("sL", "de"), ("tL",))
-        tt(T.lT[:], T.tT[:], T.oa[:], ALU.add, ("tT", "oa"), ("lT",))
-        cp(T.uT[:], T.lT[:], ("lT",), ("uT",))
-        tt(T.lL[:], T.tL[:], T.oa[:], ALU.add, ("tL", "oa"), ("lL",))
-        cp(T.uL[:], T.lL[:], ("lL",), ("uL",))
-        act(T.top[:], T.kid[:, 0:W].indirect(T.uT[:]), AF.Identity, ("kid", "uT", "sct", "bit"), ("top",), bias=C(BIT), scale=C(SCT))
+        tt(T.l2[:, 0:16], T.tT[:], T.oa[:], ALU.add, ("tT", "oa"), p=("l2",))
+        tt(T.l2[:, 16:32], T.tL[:], T.oa[:], ALU.add, ("tL", "oa"), p=("l2",))
+        cp(T.u2[:], T.l2[:], ("l2",), ("u2",))
+        for h in range(2):
+            act(T.top[:, 128 * h:128 * h + 128], T.kid[:, 0:W].indirect(T.u2[:, 8 * h:8 * h + 8]), AF.Identity, ("kid", "u2", "sct", "bit"), ("top%d" % h,),
+                bias=C(BIT), scale=C(SCT))
         ts(T.ncd[:], ev, 1.0, C(DUMP), ALU.is_lt, ALU.mult, ("es", "dump"), ("ncd",))
-        ts(T.na[:], last16(T.vI), T.limB[:], None, ALU.is_ge, None, ("vI", "limB"), ("na",))
-        if t < STEPS - 1:
+        if not final:
             ts(T.cov[:], ev, 1.0, None, ALU.is_ge, None, ("es",), ("cov",))
         tt(T.s1[:], T.oa[:], T.ncd[:], ALU.max, ("oa", "ncd"), ("s1",))
-        tt(T.cf[:], T.kid[:, 0:W].indirect(T.uL[:]), T.top[:], ALU.max, ("kid", "uL", "top"), ("cf",))
-        cp(outC(t), T.cf[:], ("cf",), (oc,))
-        wd = 272 if t < STEPS - 1 else 256
-        need("g", (oc, oo))
-        g.remote_dma(T.inC[:, 272 * t + 272:272 * t + 272 + wd], T.outC[:, 272 * t:272 * t + wd], T.sem["c%d" % (t + 1)], T.sem.ls, pid, rid, mask)
-        cnt["ls"] = cnt.get("ls", 0) + nout
+        ts(T.na[:], last16(T.vI), T.limA[:], 65536.0, ALU.subtract, ALU.is_ge, ("vI", "limA"), ("na",))
+        for h in range(2):
+            s, o = slice(128 * h, 128 * h + 128), 272 * t + 128 * h
+            e = o + (144 if h and not final else 128)
+            tt(T.cf[:, s], T.kid[:, 0:W].indirect(T.u2[:, 16 + 8 * h:24 + 8 * h]), T.top[:, s], ALU.max, ("kid", "u2", "top%d" % h), ("cf%d" % h,))
+            cp(T.outC[:, o:o + 128], T.cf[:, s], ("cf%d" % h,), ("oC%d" % h,))
+            send(T.inC[:, o + 272:e + 272], T.outC[:, o:e], "ab"[h] + "%d" % (t + 1), ("oC%d" % h, oo))
         cp(T.s1u[:], T.s1[:], ("s1",), ("s1u",))
         act(T.gl[:], T.idW[:].indirect(T.s1u[:]), AF.Copy, ("idW", "s1u"), ("gl",))
         q = 5 * t % 16
-        pr, prn = (inP(t), ic) if t else (T.prev0[:], "prev0")
+        pr, prn = (inP(t), ibn) if t else (T.prev0[:], "prev0")
         tt(T.dk[:], T.key[:], T.MK[:, q::16], ALU.subtract, ("key", "MK"), ("dk",))
         ts(T.pn[:], pr, T.CJ[:, q:q + 1], None, ALU.add, None, (prn, "CJ"), ("pn",))
         tt(T.dk2[:], T.dk[:], T.na[:], ALU.mult, ("dk", "na"), ("dk2",))
@@ -392,33 +408,38 @@ def rank_program(g, core, T, topo):
         tt(T.MK[:, q::16], T.MK[:, q::16], T.dk2[:], ALU.add, ("dk2",), ("MK",))
         tt(T.dn2[:], T.dn[:], T.na[:], ALU.mult, ("dn", "na"), ("dn2",))
         tt(T.pM[:, q:256:16], T.dn2[:], T.pM[:, q:256:16], ALU.add, ("dn2",), ("pM",))
-        if t < STEPS - 1:
-            limit()
+        lim = limit() if not final else []
+        nextlim = lambda: lim.pop(0)() if lim else None
+        nextlim()
         tt(T.eq2[:], T.s1[:].indirect(T.expl[:]), T.gl[:], ALU.is_equal, ("s1", "expl", "gl"), ("eq2",))
+        nextlim()
         scan(T.dsum[:], T.R2[:], T.eq2[:], ALU.mult, ALU.add, ("R2", "eq2"), "dsum")
+        nextlim()
         ts(T.dd[:], last16(T.dsum), C(THR), C(DUMP), ALU.is_ge, ALU.mult, ("dsum", "thr", "dump"), ("dd",))
+        nextlim()
         tt(T.s2[:], T.s1[:], T.dd[:], ALU.max, ("s1", "dd"), ("s2",))
         cp(T.s2u[:, 0::2], T.s2[:], ("s2",), ("s2u",))
     scatters()
-    yb = ["pA", "pB", "pC", "pW"]
-    for i in range(1, 8):
-        p = yb[i % 4]
-        act(T[p][:], T.kid[:, 512 * i:512 * i + 512], AF.Copy, ("kid",), (p,), scale=float(i + 1))
-        if i == 1:
-            tt(T.t1[:], T.pM[:, 0:256], T.CJ2[:], ALU.subtract, ("pM", "CJ2"), ("t1",))
-            ts(T.t2[:], T.MK[:], 1.0 / 64, None, ALU.mult, None, ("MK",), ("t2",))
-            flip((T.t1[:], "t1"), T.X, T.XT, "X")
-            flip((T.t2[:], "t2"), T.Y, T.YT, "Y")
-            for b in range(16):
-                sh = T.SH[:, 128 * (-b % 16):128 * (-b % 16) + 128]
-                for e, (XT, nx, o) in enumerate(((T.XT, "XT", 0), (T.XT, "XT", 16), (T.YT, "YT", 0), (T.YT, "YT", 16))):
-                    op("t", te.matmul, (T.pv[:, b:256:16], sh, XT[:, :, o + b], e == 0, e == 3), ("SH", nx), p=("pv",))
-            arrive("c%d" % STEPS, nin, ("inC%d" % STEPS,))
-        tt(T.acc[:], T.kid[:, 0:512] if i == 1 else T.acc[:], T[p][:], ALU.add, ("kid" if i == 1 else "acc", p), ("acc",))
-        if i == 4:
-            ts(T.yno[:], inC(STEPS), C(OFF), None, ALU.subtract, None, ("inC%d" % STEPS, "off"), ("yno",))
-            dma("y", T.yn[:], T.yno[:], "yn", r=("yno",))
+    yb = ["pA", "pB", "pC", "pW", "pX", "pL"]
+    for i in range(1, 7):
+        act(T[yb[i - 1]][:], T.kid[:, 512 * i:512 * i + 512], AF.Copy, ("kid",), (yb[i - 1],), scale=float(i + 1))
+    tt(T.mo16[:], T.pM[:, 0:256], T.CJ2[:], ALU.subtract, ("pM", "CJ2"), ("mo16",))
+    ts(T.mk16[:], T.MK[:], 1.0 / 64, None, ALU.mult, None, ("MK",), ("mk16",))
+    flip((T.mo16[:], ("mo16",)), T.X, T.XT, "X")
+    flip((T.mk16[:], ("mk16",)), T.Y, T.YT, "Y")
+    for b in range(16):
+        sh = T.SH[:, 128 * (-b % 16):128 * (-b % 16) + 128]
+        for e, (XT, nx, o) in enumerate(((T.XT, "XT", 0), (T.XT, "XT", 16), (T.YT, "YT", 0), (T.YT, "YT", 16))):
+            op("t", te.matmul, (T.pv[:, b:256:16], sh, XT[:, :, o + b], e == 0, e == 3), ("SH", nx), p=("pv",))
+    arrive("a%d" % STEPS, nin, ("inCa%d" % STEPS,))
+    arrive("b%d" % STEPS, nin, ("inCb%d" % STEPS,))
+    tt(T.acc[:], T.kid[:, 0:512], T[yb[0]][:], ALU.add, ("kid", yb[0]), ("acc",))
+    act(T[yb[0]][:], T.kid[:, 3584:4096], AF.Copy, ("kid",), (yb[0],), scale=8.0)
+    ts(T.yno[:], inC(STEPS), C(OFF), None, ALU.subtract, None, ("inCa%d" % STEPS, "inCb%d" % STEPS, "off"), ("yno",))
+    dma("y", T.yn[:], T.yno[:], "yn", r=("yno",))
     act(T.ymo[:], T.pv[:, 0:256], AF.Copy, ("pv",), ("ymo",), scale=64.0, bias=131072.0)
+    dma("s", T.ymu[:], T.ymo[:], "ymu", r=("ymo",))
+    for p in yb[1:] + yb[:1]:
+        tt(T.acc[:], T.acc[:], T[p][:], ALU.add, ("acc", p), ("acc",))
     dma("y", T.yd[:], T.acc[:], "yd", r=("acc",))
-    dma("y", T.ymu[:], T.ymo[:], "ymu", r=("ymo",))
     finish("g")

@@ -4,7 +4,8 @@ STEPS, W, L, LIM = 8, 4096, 256, 60
 CH = [(0, 2), (2, 6), (6, 10), (10, 14)]
 OWN = 14
 XF = 1
-KD, KG = 7, 3
+KD, KG = 6, 3
+NT = 11
 BIG = float(2 ** 26)
 
 _f, _b, _h, _i, _u = "float32", "bfloat16", "float16", "int32", "uint16"
@@ -21,11 +22,12 @@ SCRATCH = {
     "IN": ("sbuf", [128, 128], _b), "If": ("sbuf", [128, 128], _f), "ones": ("sbuf", [128, 128], _b), "wblk": ("sbuf", [128, 128], _b),
     "b8": ("sbuf", [128, 8], _b), "Kc": ("sbuf", [128, 256], _b), "expl": ("sbuf", [128, 16], _u),
     "RST": ("sbuf", [128, 256], _f), "RZ": ("sbuf", [128, 256], _f), "R1": ("sbuf", [128, 256], _f), "R2": ("sbuf", [128, 256], _f),
-    "CJ": ("sbuf", [128, 16], _f), "CJ2": ("sbuf", [128, 256], _f), "t3": ("sbuf", [128, 256], _f),
+    "CJ": ("sbuf", [128, 16], _f), "CJ2": ("sbuf", [128, 256], _f),
     "col": ("sbuf", [128, 16], _f), "offc": ("sbuf", [128, 16], _f), "wti": ("sbuf", [128, 1], _i), "wtf": ("sbuf", [128, 1], _f),
     "ci": ("sbuf", [128, 256], _i), "mkb": ("sbuf", [128, 256], _b), "moi": ("sbuf", [128, 256], _i), "mk16": ("sbuf", [128, 256], _h), "mo16": ("sbuf", [128, 256], _h),
     "lai": ("sbuf", [128, 16], _i), "LX": ("sbuf", [128, 32], _f), "LT": ("sbuf", [128, 32], _f), "prev0": ("sbuf", [128, 16], _f),
     "X": ("sbuf", [128, 16, 32], _h), "XT": ("sbuf", [128, 16, 32], _h), "Y": ("sbuf", [128, 16, 32], _h), "YT": ("sbuf", [128, 16, 32], _h),
+    "G": ("sbuf", [128, 8, 32], _h), "GT": ("sbuf", [128, 8, 32], _h), "PM": ("sbuf", [128, 512], _h), "S4": ("sbuf", [128, 4, 2, 16], _h),
     "MK": ("sbuf", [128, 256], _f), "Lp": ("sbuf", [128, 256], _f), "vm": ("sbuf", [128, 256], _f), "vI": ("sbuf", [128, 256], _i),
     "oa": ("sbuf", [128, 16], _i), "kk": ("sbuf", [128, 16], _i), "po": ("sbuf", [128, 16], _i), "pb": ("sbuf", [128, 16], _i), "pbb": ("sbuf", [128, 16], _i), "pu": ("sbuf", [128, 16], _u),
     "ky": ("sbuf", [128, 256], _f), "ks": ("sbuf", [128, 256], _i), "key": ("sbuf", [128, 16], _i),
@@ -40,7 +42,7 @@ SCRATCH = {
     "yno": ("sbuf", [128, 256], _f), "ymo": ("sbuf", [128, 256], _f), "acc": ("sbuf", [128, 512], _f),
     "outC": ("sbuf", [128, STEPS * 272], _u), "inC": ("sbuf", [128, (STEPS + 1) * 272], _u),
     "outW": ("sbuf", [128, STEPS * 256], _b), "inW": ("sbuf", [128, STEPS * 256], _b),
-    "pv": ("psum", [128, 512], _f), "pL": ("psum", [128, 512], _f), "pM": ("psum", [128, 512], _f), "pC": ("psum", [128, 512], _f),
+    "pv": ("psum", [128, 8, 32], _f), "pL": ("psum", [128, 8, 32], _f), "pM": ("psum", [128, 512], _f), "pC": ("psum", [128, 512], _f),
     "pW": ("psum", [128, 512], _f), "pA": ("psum", [128, 512], _f), "pB": ("psum", [128, 512], _f), "pX": ("psum", [128, 512], _f),
 }
 DMAS = ["cand", "want", "wts", "last", "mkey", "mobj", "f0", "fd", "k0", "k1", "k2", "k3", "yn", "ymu", "yd"]
@@ -254,16 +256,17 @@ def rank_program(g, core, T, topo):
     act(T.CJ2[:], T.CJ[:].indirect(T.exb[:]), AF.Copy, ("CJ", "exb"), ("CJ2",), bias=2048.0)
     cp(T.R16[:, :, 0:16], T.I16[:], ("I16",), p=("R16",))
     cp(T.R16[:, :, 16:32], T.I16[:], ("I16",), p=("R16",))
+    for s in range(2):
+        cp(T.S4[:, :, s, :], T.R16[:, 1 - s::2, 0:16], ("R16",), p=("S4",))
+    for e, m, nm in ((0, M0, "m0"), (1, M1, "m1")):
+        ts(T.PM[:, 384 * e:384 * e + 128], T.I16[:], C(m), None, ALU.mult, None, ("I16", nm), p=("PM",))
+        ts(T.PM[:, 128 + 128 * e:256 + 128 * e], T.S4[:], C(m), None, ALU.mult, None, ("S4", nm), p=("PM",))
     for b in range(16):
         cp(T.SH[:, 128 * b:128 * b + 128], T.R16[:, :, b:b + 16], ("R16",), p=("SH",))
 
-    def flip(src, X, XT, nx, cen=None):
+    def flip(src, ns, X, XT, nx):
         for h, m, nm in ((0, M0, "m0"), (1, M1, "m1")):
-            o = X[:, :, 16 * h:16 * h + 16]
-            if cen is None:
-                ts(o, src[0], C(m), None, ALU.mult, None, src[1] + (nm,), p=(nx,))
-            else:
-                ts(o, src[0], cen[0], C(m), ALU.subtract, ALU.mult, src[1] + (nm, cen[1]), p=(nx,))
+            ts(X[:, :, 16 * h:16 * h + 16], src, C(m), None, ALU.mult, None, (ns, nm), p=(nx,))
         op("v", v.transpose, (XT[:], X[:]), (nx,), (nx + "T",))
 
     def halves(out, XT, nx, w):
@@ -274,16 +277,16 @@ def rank_program(g, core, T, topo):
     for ps, src in (("pA", "mk16"), ("pB", "mo16")):
         for b in range(16):
             op("t", te.matmul, (T[ps][:, b:256:16], T.SH[:, 128 * b:128 * b + 128], T[src][:, b::16], True, True), ("SH", src), p=(ps,))
-    flip((T.pA[:, 0:256], ("pA",)), T.X, T.XT, "X")
-    flip((T.pB[:, 0:256], ("pB",)), T.Y, T.YT, "Y")
+    flip(T.pA[:, 0:256], "pA", T.X, T.XT, "X")
+    flip(T.pB[:, 0:256], "pB", T.Y, T.YT, "Y")
     halves(T.pA[:, 0:256], T.XT, "X", "pA")
     halves(T.pB[:, 0:256], T.YT, "Y", "pB")
     ts(T.LX[:, 0:16], T.lai[:], C(M0), None, ALU.mult, None, ("lai", "m0"), p=("LX",))
     ts(T.LX[:, 16:32], T.lai[:], C(M1), None, ALU.mult, None, ("lai", "m1"), p=("LX",))
     op("v", v.transpose, (T.LT[:], T.LX[:]), ("LX",), ("LT",))
     tt(T.prev0[:], T.LT[:, 0:16], T.LT[:, 16:32], ALU.add, ("LT",), ("prev0",))
-    scan(T.t3[:], T.R2[:], T.diag[:], ALU.mult, ALU.add, ("R2", "diag"), "t3")
-    ts(C(THR), T.t3[:, 15:16], 2.0, None, ALU.mult, None, ("t3",), ("thr",))
+    scan(T.dsum[:], T.R2[:], T.diag[:], ALU.mult, ALU.add, ("R2", "diag"), "dsum")
+    ts(C(THR), T.dsum[:, 15:16], 2.0, None, ALU.mult, None, ("dsum",), ("thr",))
     ts(T.offc[:], T.dg[:], 0.0, C(OFF), ALU.mult, ALU.add, ("dg", "off"), ("offc",))
     act(T.MK[:], T.pA[:, 0:256], AF.Copy, ("pA",), ("MK",))
     tt(T.pM[:, 0:256], T.pB[:, 0:256], T.CJ2[:], ALU.add, ("pB", "CJ2"), ("pM",))
@@ -299,38 +302,39 @@ def rank_program(g, core, T, topo):
             p = kbank[i % 4]
             act(T.keyW[:, 512 * i:512 * i + 512], T[p][:], AF.Copy, (p,), p=("keyW",))
 
+    scq = []
+
     def scatters():
-        for c in range(15, -1, -1):
+        scq.extend(range(15, -1, -1))
+
+    def scatter(k=1):
+        for i in range(min(k, len(scq))):
+            c = scq.pop(0)
             tt(T.kid[:].indirect(T.s2u[:, 2 * c:2 * c + 1]), T.cf[:, 16 * c:16 * c + 16], T.offc[:], ALU.subtract, ("s2u", "cf0", "cf1", "offc"), ("kid",))
 
     def limit():
         mm(T.pC[:, 0:16], T.ones[:], T.cov[:], True, True, ("ones", "cov"), "pC")
-        return [lambda: op("v", v.tensor_reduce, (T.cs[:], T.pC[:, 0:16], AxisListType.X, ALU.add), ("pC",), ("cs",)),
+        return [lambda: op("v", v.tensor_reduce, (T.cs[:], T.pC[:, 0:16], AxisListType.X, ALU.add), ("pC",), ("cs",), kw=dict(negate=True)),
                 lambda: cp(T.csi[:], T.cs[:], ("cs",), ("csi",)),
                 lambda: ts(T.csa[:], T.csi[:], 15, None, ALU.bitwise_and, None, ("csi",), ("csa",)),
                 lambda: ts(T.limA[:], T.csa[:], 65536.0, 65536.0 * (LIM - 1), ALU.mult, ALU.add, ("csa",), ("limA",))]
 
     def dist(c0, c1, nm, stop):
         for b in range(16):
-            mm(T.pv[:, 16 * c0:16 * c1], T.LH[:, 128 * b:128 * b + 128], T.A[:, c0:c1, 16 * b:16 * b + 16], False, stop and b == 15, ("LH", nm), "pv")
+            mm(T.pv[:, c0 // 2:c1 // 2, :], T.LH[:, 128 * b:128 * b + 128], T.A[:, c0:c1, 16 * b:16 * b + 16], False, stop and b == 15, ("LH", nm), "pv")
     keys(0)
     for t in range(STEPS):
         iw, ia, ibn, final = "inW%d" % t, "inCa%d" % t, "inCb%d" % t, t == STEPS - 1
-        if t:
-            arrive("w%d" % t, nin, (iw,))
-            arrive("a%d" % t, nin, (ia,))
-            arrive("b%d" % t, nin, (ibn,))
-            for k in range(16):
-                expand(t, "v" if k < KD else "s" if k < 16 - KG else "g", k)
         fw = 2 * W if t else W
         fr = ("feat", "featd") if t else ("feat",)
-        mm(T.pv[:, 0:256], T.IB[:], T.Kc[:], True, False, ("IB", "Kc"), "pv")
-        mm(T.pL[:, 0:256], T.IB[:], T.Kc[:], True, False, ("IB", "Kc"), "pL")
+        mm(T.pv[:], T.IB[:], T.Kc[:], True, False, ("IB", "Kc"), "pv")
+        mm(T.pL[:], T.IB[:], T.Kc[:], True, False, ("IB", "Kc"), "pL")
         for x, (c0, c1) in enumerate(CH):
             tt(T.D[:, 256 * c0:256 * c1], T.featW[:, 0:fw].indirect(T.inC[:, 272 * t + 16 * c0:272 * t + 16 * c1]), T.Wx[:, 256 * c0:256 * c1], ALU.subtract,
                fr + ("Wx", ia) + ((ibn,) if c1 > 8 else ()), ("D%d" % x,))
             if x == XF:
-                flip((inC(t), (ia, ibn)), T.X, T.XT, "X", (C(CEN if t else CEN0), "cen" if t else "cen0"))
+                ts(T.G[:], inC(t), C(CEN if t else CEN0), None, ALU.subtract, None, (ia, ibn, "cen" if t else "cen0"), ("G",))
+                op("v", v.transpose, (T.GT[:], T.G[:]), ("G",), ("GT",))
             if x == 0:
                 act(T.raw[:], T.featW[:, 0:fw].indirect(T.inC[:, 272 * t + 16 * OWN:272 * t + 256]), AF.Copy, fr + (ibn,), ("raw",))
                 mm(T.pX[:], T.IB[:], T.raw[:], True, False, ("IB", "raw"), "pX")
@@ -339,13 +343,15 @@ def rank_program(g, core, T, topo):
             if x == 1:
                 act(T.A[:, OWN:16, :], T.pX[:], AF.Abs, ("pX",), ("A9",))
             if x == 2:
-                act(T.Lp[:], T.pL[:, 0:256], AF.Identity, ("pL", "limA"), ("Lp",), bias=T.limA[:])
+                act(T.Lp[:], T.pL[:], AF.Identity, ("pL", "limA"), ("Lp",), bias=T.limA[:])
             if x == len(CH) - 1 and not final:
                 act(T.D[:, 256 * OWN:4096], T.pX[:], AF.Abs, ("pX",), ("D9",))
             if x == XF:
                 for p, e in (("pL", True), ("pv", False)):
-                    mm(T[p][:, 0:256], T.I16[:], T.XT[:, :, 0:16], False, False, ("I16", "XT"), p)
-                    mm(T[p][:, 0:256], T.I16[:], T.XT[:, :, 16:32], False, e, ("I16", "XT"), p)
+                    for c in range(2):
+                        for s in range(2):
+                            o = 256 * c + 128 * s
+                            mm(T[p][:, :, 16 * c:16 * c + 16], T.PM[:, o:o + 128], T.GT[:, :, 16 * s:16 * s + 16], False, e and c + s == 2, ("PM", "GT"), p)
             dist(c0, c1, "A%d" % x, x == len(CH) - 1)
             if x == 1:
                 dist(OWN, 16, "A9", False)
@@ -355,91 +361,118 @@ def rank_program(g, core, T, topo):
                 cp(T.kid[:, 1024 * q:1024 * q + 1024], T.kidi[:, 1024 * q:1024 * q + 1024], ("kidi%d" % q,), p=("kid",))
         else:
             scatters()
-        tt(T.vm[:], T.pv[:, 0:256], T.Lp[:], ALU.max, ("pv", "Lp"), ("vm",))
+            scatter(NT)
+        tt(T.vm[:], T.pv[:], T.Lp[:], ALU.max, ("pv", "Lp"), ("vm",))
+        scatter()
         scan(T.vI[:], T.RST[:], T.vm[:], ALU.max, ALU.min, ("RST", "vm"), "vI")
+        scatter()
         ts(T.oa[:], last16(T.vI), 4095, None, ALU.bitwise_and, None, ("vI",), ("oa",))
         oo = "outO%d" % t
         if not final:
             ts(T.kk[:], last16(T.vI), 12, 15, ALU.logical_shift_right, ALU.bitwise_and, ("vI",), ("kk",))
+        scatter()
         cp(outO(t), T.oa[:], ("oa",), (oo,))
         if not final:
             tt(T.po[:], T.kk[:], T.pb[:], ALU.add, ("kk", "pb"), ("po",))
+        tt(T.ky[:], T.keyW[:].indirect(outO(t)), T.diag[:], ALU.mult, ("keyW", oo, "diag"), ("ky",))
+        if not final:
             cp(T.pu[:], T.po[:], ("po",), ("pu",))
             act(outW(t), T.D[:].indirect(T.pu[:]), AF.Abs, tuple("D%d" % x for x in range(len(CH))) + ("D9", "pu"), ("outW%d" % t,))
             send(inW(t + 1), outW(t), "w%d" % (t + 1), ("outW%d" % t,))
-        tt(T.ky[:], T.keyW[:].indirect(outO(t)), T.diag[:], ALU.mult, ("keyW", oo, "diag"), ("ky",))
+        scatter()
         scan(T.ks[:], T.R1[:], T.ky[:], ALU.mult, ALU.add, ("R1", "ky"), "ks")
+        scatter()
         ts(T.key[:], last16(T.ks), 63, None, ALU.bitwise_and, None, ("ks",), ("key",))
+        scatter()
         tt(T.eq[:], T.key[:].indirect(T.expl[:]), T.MK[:], ALU.is_equal, ("key", "expl", "MK"), ("eq",))
+        scatter()
         tt(T.em[:], T.eq[:], T.pM[:, 0:256], ALU.mult, ("eq", "pM"), ("em",))
+        scatter(16)
         scan(T.es[:], T.RZ[:], T.em[:], ALU.min, ALU.max, ("RZ", "em"), "es")
         ev = last16(T.es)
         ts(T.eo[:], ev, 4095, None, ALU.bitwise_and, None, ("es",), ("eo",))
         ts(T.sT[:], ev, 13, 1, ALU.logical_shift_right, ALU.bitwise_and, ("es",), ("sT",))
         ts(T.sL[:], ev, 12, 1, ALU.logical_shift_right, ALU.bitwise_and, ("es",), ("sL",))
         tt(T.de[:], T.eo[:], T.oa[:], ALU.subtract, ("eo", "oa"), ("de",))
+        ts(T.ncd[:], ev, 1.0, C(DUMP), ALU.is_lt, ALU.mult, ("es", "dump"), ("ncd",))
         tt(T.tT[:], T.sT[:], T.de[:], ALU.mult, ("sT", "de"), ("tT",))
         tt(T.tL[:], T.sL[:], T.de[:], ALU.mult, ("sL", "de"), ("tL",))
         tt(T.l2[:, 0:16], T.tT[:], T.oa[:], ALU.add, ("tT", "oa"), p=("l2",))
         tt(T.l2[:, 16:32], T.tL[:], T.oa[:], ALU.add, ("tL", "oa"), p=("l2",))
+        ts(T.na[:], last16(T.vI), T.limA[:], 65536.0, ALU.subtract, ALU.is_ge, ("vI", "limA"), ("na",))
         cp(T.u2[:], T.l2[:], ("l2",), ("u2",))
         for h in range(2):
             act(T.top[:, 128 * h:128 * h + 128], T.kid[:, 0:W].indirect(T.u2[:, 8 * h:8 * h + 8]), AF.Identity, ("kid", "u2", "sct", "bit"), ("top%d" % h,),
                 bias=C(BIT), scale=C(SCT))
-        ts(T.ncd[:], ev, 1.0, C(DUMP), ALU.is_lt, ALU.mult, ("es", "dump"), ("ncd",))
-        if not final:
-            ts(T.cov[:], ev, 1.0, None, ALU.is_ge, None, ("es",), ("cov",))
+        q = 5 * t % 16
+        pr, prn = (inP(t), ibn) if t else (T.prev0[:], "prev0")
+        tt(T.dk[:], T.key[:], T.MK[:, q::16], ALU.subtract, ("key", "MK"), ("dk",))
         tt(T.s1[:], T.oa[:], T.ncd[:], ALU.max, ("oa", "ncd"), ("s1",))
-        ts(T.na[:], last16(T.vI), T.limA[:], 65536.0, ALU.subtract, ALU.is_ge, ("vI", "limA"), ("na",))
+        ts(T.pn[:], pr, T.CJ[:, q:q + 1], None, ALU.add, None, (prn, "CJ"), ("pn",))
+        tt(T.dk2[:], T.dk[:], T.na[:], ALU.mult, ("dk", "na"), ("dk2",))
+        cp(T.s1u[:], T.s1[:], ("s1",), ("s1u",))
+        tt(T.dn[:], T.pn[:], T.pM[:, q:256:16], ALU.subtract, ("pn", "pM"), ("dn",))
         for h in range(2):
             s, o = slice(128 * h, 128 * h + 128), 272 * t + 128 * h
             e = o + (144 if h and not final else 128)
             tt(T.cf[:, s], T.kid[:, 0:W].indirect(T.u2[:, 16 + 8 * h:24 + 8 * h]), T.top[:, s], ALU.max, ("kid", "u2", "top%d" % h), ("cf%d" % h,))
+            if h == 0:
+                tt(T.MK[:, q::16], T.MK[:, q::16], T.dk2[:], ALU.add, ("dk2",), ("MK",))
+                tt(T.dn2[:], T.dn[:], T.na[:], ALU.mult, ("dn", "na"), ("dn2",))
+            else:
+                tt(T.pM[:, q:256:16], T.dn2[:], T.pM[:, q:256:16], ALU.add, ("dn2",), ("pM",))
             cp(T.outC[:, o:o + 128], T.cf[:, s], ("cf%d" % h,), ("oC%d" % h,))
             send(T.inC[:, o + 272:e + 272], T.outC[:, o:e], "ab"[h] + "%d" % (t + 1), ("oC%d" % h, oo))
-        cp(T.s1u[:], T.s1[:], ("s1",), ("s1u",))
+        if not final:
+            act(T.cov[:], T.ncd[:], AF.Sign, ("ncd",), ("cov",))
         act(T.gl[:], T.idW[:].indirect(T.s1u[:]), AF.Copy, ("idW", "s1u"), ("gl",))
-        q = 5 * t % 16
-        pr, prn = (inP(t), ibn) if t else (T.prev0[:], "prev0")
-        tt(T.dk[:], T.key[:], T.MK[:, q::16], ALU.subtract, ("key", "MK"), ("dk",))
-        ts(T.pn[:], pr, T.CJ[:, q:q + 1], None, ALU.add, None, (prn, "CJ"), ("pn",))
-        tt(T.dk2[:], T.dk[:], T.na[:], ALU.mult, ("dk", "na"), ("dk2",))
-        tt(T.dn[:], T.pn[:], T.pM[:, q:256:16], ALU.subtract, ("pn", "pM"), ("dn",))
-        tt(T.MK[:, q::16], T.MK[:, q::16], T.dk2[:], ALU.add, ("dk2",), ("MK",))
-        tt(T.dn2[:], T.dn[:], T.na[:], ALU.mult, ("dn", "na"), ("dn2",))
-        tt(T.pM[:, q:256:16], T.dn2[:], T.pM[:, q:256:16], ALU.add, ("dn2",), ("pM",))
-        lim = limit() if not final else []
-        nextlim = lambda: lim.pop(0)() if lim else None
-        nextlim()
+        lim, wq = [], []
+        if final:
+            tt(T.mo16[:], T.pM[:, 0:256], T.CJ2[:], ALU.subtract, ("pM", "CJ2"), ("mo16",))
+            ts(T.mk16[:], T.MK[:], 1.0 / 64, None, ALU.mult, None, ("MK",), ("mk16",))
+            flip(T.mo16[:], "mo16", T.X, T.XT, "X")
+            flip(T.mk16[:], "mk16", T.Y, T.YT, "Y")
+            for b in range(16):
+                sh = T.SH[:, 128 * (-b % 16):128 * (-b % 16) + 128]
+                for e, (XT, nx, o) in enumerate(((T.XT, "XT", 0), (T.XT, "XT", 16), (T.YT, "YT", 0), (T.YT, "YT", 16))):
+                    op("t", te.matmul, (T.pA[:, b:256:16], sh, XT[:, :, o + b], e == 0, e == 3), ("SH", nx), p=("pA",))
+        else:
+            lim = limit()
+            arrive("w%d" % (t + 1), nin, ("inW%d" % (t + 1),))
+            arrive("a%d" % (t + 1), nin, ("inCa%d" % (t + 1),))
+            arrive("b%d" % (t + 1), nin, ("inCb%d" % (t + 1),))
+            for k in range(KD, 16):
+                expand(t + 1, "s" if k < 16 - KG else "g", k)
+            wq = list(range(KD))
+        fill_in = lambda: lim.pop(0)() if lim else expand(t + 1, "v", wq.pop(0)) if wq else None
+        fill_in()
         tt(T.eq2[:], T.s1[:].indirect(T.expl[:]), T.gl[:], ALU.is_equal, ("s1", "expl", "gl"), ("eq2",))
-        nextlim()
+        fill_in()
         scan(T.dsum[:], T.R2[:], T.eq2[:], ALU.mult, ALU.add, ("R2", "eq2"), "dsum")
-        nextlim()
+        fill_in()
         ts(T.dd[:], last16(T.dsum), C(THR), C(DUMP), ALU.is_ge, ALU.mult, ("dsum", "thr", "dump"), ("dd",))
-        nextlim()
+        fill_in()
         tt(T.s2[:], T.s1[:], T.dd[:], ALU.max, ("s1", "dd"), ("s2",))
+        fill_in()
         cp(T.s2u[:, 0::2], T.s2[:], ("s2",), ("s2u",))
+        while wq:
+            fill_in()
     scatters()
-    yb = ["pA", "pB", "pC", "pW", "pX", "pL"]
-    for i in range(1, 7):
+    scatter(16)
+    yb = ["pB", "pC", "pW", "pX"]
+    for i in range(1, 5):
         act(T[yb[i - 1]][:], T.kid[:, 512 * i:512 * i + 512], AF.Copy, ("kid",), (yb[i - 1],), scale=float(i + 1))
-    tt(T.mo16[:], T.pM[:, 0:256], T.CJ2[:], ALU.subtract, ("pM", "CJ2"), ("mo16",))
-    ts(T.mk16[:], T.MK[:], 1.0 / 64, None, ALU.mult, None, ("MK",), ("mk16",))
-    flip((T.mo16[:], ("mo16",)), T.X, T.XT, "X")
-    flip((T.mk16[:], ("mk16",)), T.Y, T.YT, "Y")
-    for b in range(16):
-        sh = T.SH[:, 128 * (-b % 16):128 * (-b % 16) + 128]
-        for e, (XT, nx, o) in enumerate(((T.XT, "XT", 0), (T.XT, "XT", 16), (T.YT, "YT", 0), (T.YT, "YT", 16))):
-            op("t", te.matmul, (T.pv[:, b:256:16], sh, XT[:, :, o + b], e == 0, e == 3), ("SH", nx), p=("pv",))
     arrive("a%d" % STEPS, nin, ("inCa%d" % STEPS,))
     arrive("b%d" % STEPS, nin, ("inCb%d" % STEPS,))
     tt(T.acc[:], T.kid[:, 0:512], T[yb[0]][:], ALU.add, ("kid", yb[0]), ("acc",))
-    act(T[yb[0]][:], T.kid[:, 3584:4096], AF.Copy, ("kid",), (yb[0],), scale=8.0)
     ts(T.yno[:], inC(STEPS), C(OFF), None, ALU.subtract, None, ("inCa%d" % STEPS, "inCb%d" % STEPS, "off"), ("yno",))
     dma("y", T.yn[:], T.yno[:], "yn", r=("yno",))
-    act(T.ymo[:], T.pv[:, 0:256], AF.Copy, ("pv",), ("ymo",), scale=64.0, bias=131072.0)
+    act(T.ymo[:], T.pA[:, 0:256], AF.Copy, ("pA",), ("ymo",), scale=64.0, bias=131072.0)
     dma("s", T.ymu[:], T.ymo[:], "ymu", r=("ymo",))
-    for p in yb[1:] + yb[:1]:
+    for i in range(2, 8):
+        p = yb[(i - 1) % 4]
+        if i > 4:
+            act(T[p][:], T.kid[:, 512 * i:512 * i + 512], AF.Copy, ("kid",), (p,), scale=float(i + 1))
         tt(T.acc[:], T.acc[:], T[p][:], ALU.add, ("acc", p), ("acc",))
     dma("y", T.yd[:], T.acc[:], "yd", r=("acc",))
     finish("g")

@@ -5,7 +5,7 @@ CH = [(0, 2), (2, 6), (6, 10), (10, 14)]
 OWN = 14
 XF = 1
 KD, KG = 6, 3
-NT = 11
+NT = 6
 BIG = float(2 ** 26)
 
 _f, _b, _h, _i, _u = "float32", "bfloat16", "float16", "int32", "uint16"
@@ -264,10 +264,10 @@ def rank_program(g, core, T, topo):
     for b in range(16):
         cp(T.SH[:, 128 * b:128 * b + 128], T.R16[:, :, b:b + 16], ("R16",), p=("SH",))
 
-    def flip(src, ns, X, XT, nx):
-        for h, m, nm in ((0, M0, "m0"), (1, M1, "m1")):
-            ts(X[:, :, 16 * h:16 * h + 16], src, C(m), None, ALU.mult, None, (ns, nm), p=(nx,))
-        op("v", v.transpose, (XT[:], X[:]), (nx,), (nx + "T",))
+    def flip_calls(src, ns, X, XT, nx):
+        return [lambda: ts(X[:, :, 0:16], src, C(M0), None, ALU.mult, None, (ns, "m0"), p=(nx,)),
+                lambda: ts(X[:, :, 16:32], src, C(M1), None, ALU.mult, None, (ns, "m1"), p=(nx,)),
+                lambda: op("v", v.transpose, (XT[:], X[:]), (nx,), (nx + "T",))]
 
     def halves(out, XT, nx, w):
         mm(out, T.I16[:], XT[:, :, 0:16], True, False, ("I16", nx + "T"), w)
@@ -277,8 +277,8 @@ def rank_program(g, core, T, topo):
     for ps, src in (("pA", "mk16"), ("pB", "mo16")):
         for b in range(16):
             op("t", te.matmul, (T[ps][:, b:256:16], T.SH[:, 128 * b:128 * b + 128], T[src][:, b::16], True, True), ("SH", src), p=(ps,))
-    flip(T.pA[:, 0:256], "pA", T.X, T.XT, "X")
-    flip(T.pB[:, 0:256], "pB", T.Y, T.YT, "Y")
+    for f in flip_calls(T.pA[:, 0:256], "pA", T.X, T.XT, "X") + flip_calls(T.pB[:, 0:256], "pB", T.Y, T.YT, "Y"):
+        f()
     halves(T.pA[:, 0:256], T.XT, "X", "pA")
     halves(T.pB[:, 0:256], T.YT, "Y", "pB")
     ts(T.LX[:, 0:16], T.lai[:], C(M0), None, ALU.mult, None, ("lai", "m0"), p=("LX",))
@@ -334,6 +334,7 @@ def rank_program(g, core, T, topo):
                fr + ("Wx", ia) + ((ibn,) if c1 > 8 else ()), ("D%d" % x,))
             if x == XF:
                 ts(T.G[:], inC(t), C(CEN if t else CEN0), None, ALU.subtract, None, (ia, ibn, "cen" if t else "cen0"), ("G",))
+                scatter()
                 op("v", v.transpose, (T.GT[:], T.G[:]), ("G",), ("GT",))
             if x == 0:
                 act(T.raw[:], T.featW[:, 0:fw].indirect(T.inC[:, 272 * t + 16 * OWN:272 * t + 256]), AF.Copy, fr + (ibn,), ("raw",))
@@ -360,7 +361,6 @@ def rank_program(g, core, T, topo):
             for q in range(4):
                 cp(T.kid[:, 1024 * q:1024 * q + 1024], T.kidi[:, 1024 * q:1024 * q + 1024], ("kidi%d" % q,), p=("kid",))
         else:
-            scatters()
             scatter(NT)
         tt(T.vm[:], T.pv[:], T.Lp[:], ALU.max, ("pv", "Lp"), ("vm",))
         scatter()
@@ -374,6 +374,7 @@ def rank_program(g, core, T, topo):
         cp(outO(t), T.oa[:], ("oa",), (oo,))
         if not final:
             tt(T.po[:], T.kk[:], T.pb[:], ALU.add, ("kk", "pb"), ("po",))
+        scatter()
         tt(T.ky[:], T.keyW[:].indirect(outO(t)), T.diag[:], ALU.mult, ("keyW", oo, "diag"), ("ky",))
         if not final:
             cp(T.pu[:], T.po[:], ("po",), ("pu",))
@@ -387,56 +388,49 @@ def rank_program(g, core, T, topo):
         tt(T.eq[:], T.key[:].indirect(T.expl[:]), T.MK[:], ALU.is_equal, ("key", "expl", "MK"), ("eq",))
         scatter()
         tt(T.em[:], T.eq[:], T.pM[:, 0:256], ALU.mult, ("eq", "pM"), ("em",))
-        scatter(16)
+        scatter()
         scan(T.es[:], T.RZ[:], T.em[:], ALU.min, ALU.max, ("RZ", "em"), "es")
+        scatter(16)
         ev = last16(T.es)
         ts(T.eo[:], ev, 4095, None, ALU.bitwise_and, None, ("es",), ("eo",))
         ts(T.sT[:], ev, 13, 1, ALU.logical_shift_right, ALU.bitwise_and, ("es",), ("sT",))
         ts(T.sL[:], ev, 12, 1, ALU.logical_shift_right, ALU.bitwise_and, ("es",), ("sL",))
         tt(T.de[:], T.eo[:], T.oa[:], ALU.subtract, ("eo", "oa"), ("de",))
+        q = 5 * t % 16
+        pr, prn = (inP(t), ibn) if t else (T.prev0[:], "prev0")
         ts(T.ncd[:], ev, 1.0, C(DUMP), ALU.is_lt, ALU.mult, ("es", "dump"), ("ncd",))
+        tt(T.dk[:], T.key[:], T.MK[:, q::16], ALU.subtract, ("key", "MK"), ("dk",))
         tt(T.tT[:], T.sT[:], T.de[:], ALU.mult, ("sT", "de"), ("tT",))
         tt(T.tL[:], T.sL[:], T.de[:], ALU.mult, ("sL", "de"), ("tL",))
+        ts(T.pn[:], pr, T.CJ[:, q:q + 1], None, ALU.add, None, (prn, "CJ"), ("pn",))
+        ts(T.na[:], last16(T.vI), T.limA[:], 65536.0, ALU.subtract, ALU.is_ge, ("vI", "limA"), ("na",))
         tt(T.l2[:, 0:16], T.tT[:], T.oa[:], ALU.add, ("tT", "oa"), p=("l2",))
         tt(T.l2[:, 16:32], T.tL[:], T.oa[:], ALU.add, ("tL", "oa"), p=("l2",))
-        ts(T.na[:], last16(T.vI), T.limA[:], 65536.0, ALU.subtract, ALU.is_ge, ("vI", "limA"), ("na",))
+        tt(T.s1[:], T.oa[:], T.ncd[:], ALU.max, ("oa", "ncd"), ("s1",))
+        tt(T.dk2[:], T.dk[:], T.na[:], ALU.mult, ("dk", "na"), ("dk2",))
         cp(T.u2[:], T.l2[:], ("l2",), ("u2",))
         for h in range(2):
             act(T.top[:, 128 * h:128 * h + 128], T.kid[:, 0:W].indirect(T.u2[:, 8 * h:8 * h + 8]), AF.Identity, ("kid", "u2", "sct", "bit"), ("top%d" % h,),
                 bias=C(BIT), scale=C(SCT))
-        q = 5 * t % 16
-        pr, prn = (inP(t), ibn) if t else (T.prev0[:], "prev0")
-        tt(T.dk[:], T.key[:], T.MK[:, q::16], ALU.subtract, ("key", "MK"), ("dk",))
-        tt(T.s1[:], T.oa[:], T.ncd[:], ALU.max, ("oa", "ncd"), ("s1",))
-        ts(T.pn[:], pr, T.CJ[:, q:q + 1], None, ALU.add, None, (prn, "CJ"), ("pn",))
-        tt(T.dk2[:], T.dk[:], T.na[:], ALU.mult, ("dk", "na"), ("dk2",))
-        cp(T.s1u[:], T.s1[:], ("s1",), ("s1u",))
         tt(T.dn[:], T.pn[:], T.pM[:, q:256:16], ALU.subtract, ("pn", "pM"), ("dn",))
+        cp(T.s1u[:], T.s1[:], ("s1",), ("s1u",))
+        tt(T.MK[:, q::16], T.MK[:, q::16], T.dk2[:], ALU.add, ("dk2",), ("MK",))
+        tt(T.dn2[:], T.dn[:], T.na[:], ALU.mult, ("dn", "na"), ("dn2",))
         for h in range(2):
-            s, o = slice(128 * h, 128 * h + 128), 272 * t + 128 * h
-            e = o + (144 if h and not final else 128)
+            s = slice(128 * h, 128 * h + 128)
             tt(T.cf[:, s], T.kid[:, 0:W].indirect(T.u2[:, 16 + 8 * h:24 + 8 * h]), T.top[:, s], ALU.max, ("kid", "u2", "top%d" % h), ("cf%d" % h,))
-            if h == 0:
-                tt(T.MK[:, q::16], T.MK[:, q::16], T.dk2[:], ALU.add, ("dk2",), ("MK",))
-                tt(T.dn2[:], T.dn[:], T.na[:], ALU.mult, ("dn", "na"), ("dn2",))
-            else:
+        for h in range(2):
+            o = 272 * t + 128 * h
+            e = o + (144 if h and not final else 128)
+            if h:
                 tt(T.pM[:, q:256:16], T.dn2[:], T.pM[:, q:256:16], ALU.add, ("dn2",), ("pM",))
-            cp(T.outC[:, o:o + 128], T.cf[:, s], ("cf%d" % h,), ("oC%d" % h,))
+            cp(T.outC[:, o:o + 128], T.cf[:, 128 * h:128 * h + 128], ("cf%d" % h,), ("oC%d" % h,))
             send(T.inC[:, o + 272:e + 272], T.outC[:, o:e], "ab"[h] + "%d" % (t + 1), ("oC%d" % h, oo))
         if not final:
             act(T.cov[:], T.ncd[:], AF.Sign, ("ncd",), ("cov",))
         act(T.gl[:], T.idW[:].indirect(T.s1u[:]), AF.Copy, ("idW", "s1u"), ("gl",))
         lim, wq = [], []
-        if final:
-            tt(T.mo16[:], T.pM[:, 0:256], T.CJ2[:], ALU.subtract, ("pM", "CJ2"), ("mo16",))
-            ts(T.mk16[:], T.MK[:], 1.0 / 64, None, ALU.mult, None, ("MK",), ("mk16",))
-            flip(T.mo16[:], "mo16", T.X, T.XT, "X")
-            flip(T.mk16[:], "mk16", T.Y, T.YT, "Y")
-            for b in range(16):
-                sh = T.SH[:, 128 * (-b % 16):128 * (-b % 16) + 128]
-                for e, (XT, nx, o) in enumerate(((T.XT, "XT", 0), (T.XT, "XT", 16), (T.YT, "YT", 0), (T.YT, "YT", 16))):
-                    op("t", te.matmul, (T.pA[:, b:256:16], sh, XT[:, :, o + b], e == 0, e == 3), ("SH", nx), p=("pA",))
-        else:
+        if not final:
             lim = limit()
             arrive("w%d" % (t + 1), nin, ("inW%d" % (t + 1),))
             arrive("a%d" % (t + 1), nin, ("inCa%d" % (t + 1),))
@@ -444,7 +438,11 @@ def rank_program(g, core, T, topo):
             for k in range(KD, 16):
                 expand(t + 1, "s" if k < 16 - KG else "g", k)
             wq = list(range(KD))
-        fill_in = lambda: lim.pop(0)() if lim else expand(t + 1, "v", wq.pop(0)) if wq else None
+        def fill_in():
+            if lim:
+                lim.pop(0)()
+            if wq:
+                expand(t + 1, "v", wq.pop(0))
         fill_in()
         tt(T.eq2[:], T.s1[:].indirect(T.expl[:]), T.gl[:], ALU.is_equal, ("s1", "expl", "gl"), ("eq2",))
         fill_in()
@@ -455,16 +453,27 @@ def rank_program(g, core, T, topo):
         tt(T.s2[:], T.s1[:], T.dd[:], ALU.max, ("s1", "dd"), ("s2",))
         fill_in()
         cp(T.s2u[:, 0::2], T.s2[:], ("s2",), ("s2u",))
+        scatters()
         while wq:
             fill_in()
-    scatters()
+        if not final:
+            scatter()
+    calls = [lambda: tt(T.mo16[:], T.pM[:, 0:256], T.CJ2[:], ALU.subtract, ("pM", "CJ2"), ("mo16",)),
+             lambda: ts(T.mk16[:], T.MK[:], 1.0 / 64, None, ALU.mult, None, ("MK",), ("mk16",))]
+    for f in calls + flip_calls(T.mo16[:], "mo16", T.X, T.XT, "X") + flip_calls(T.mk16[:], "mk16", T.Y, T.YT, "Y"):
+        scatter()
+        f()
+    for b in range(16):
+        sh = T.SH[:, 128 * (-b % 16):128 * (-b % 16) + 128]
+        for e, (XT, nx, o) in enumerate(((T.XT, "XT", 0), (T.XT, "XT", 16), (T.YT, "YT", 0), (T.YT, "YT", 16))):
+            op("t", te.matmul, (T.pA[:, b:256:16], sh, XT[:, :, o + b], e == 0, e == 3), ("SH", nx), p=("pA",))
     scatter(16)
     yb = ["pB", "pC", "pW", "pX"]
     for i in range(1, 5):
         act(T[yb[i - 1]][:], T.kid[:, 512 * i:512 * i + 512], AF.Copy, ("kid",), (yb[i - 1],), scale=float(i + 1))
     arrive("a%d" % STEPS, nin, ("inCa%d" % STEPS,))
     arrive("b%d" % STEPS, nin, ("inCb%d" % STEPS,))
-    tt(T.acc[:], T.kid[:, 0:512], T[yb[0]][:], ALU.add, ("kid", yb[0]), ("acc",))
+    tt(T.acc[:], T.kid[:, 0:512], T[yb[0]][:], ALU.add, ("kid", yb[0]), ("acc0", "acc1"))
     ts(T.yno[:], inC(STEPS), C(OFF), None, ALU.subtract, None, ("inCa%d" % STEPS, "inCb%d" % STEPS, "off"), ("yno",))
     dma("y", T.yn[:], T.yno[:], "yn", r=("yno",))
     act(T.ymo[:], T.pA[:, 0:256], AF.Copy, ("pA",), ("ymo",), scale=64.0, bias=131072.0)
@@ -473,6 +482,8 @@ def rank_program(g, core, T, topo):
         p = yb[(i - 1) % 4]
         if i > 4:
             act(T[p][:], T.kid[:, 512 * i:512 * i + 512], AF.Copy, ("kid",), (p,), scale=float(i + 1))
-        tt(T.acc[:], T.acc[:], T[p][:], ALU.add, ("acc", p), ("acc",))
-    dma("y", T.yd[:], T.acc[:], "yd", r=("acc",))
+        for h in range(2):
+            s, a = slice(256 * h, 256 * h + 256), "acc%d" % h
+            tt(T.acc[:, s], T.acc[:, s], T[p][:, s], ALU.add, (a, p), (a,))
+    dma("y", T.yd[:], T.acc[:], "yd", r=("acc0", "acc1"))
     finish("g")

from concourse.mybir import AluOpType as ALU, AxisListType, ActivationFunctionType as AF

STEPS, W, L, LIM = 8, 4096, 256, 60
CH = [(0, 2), (2, 6), (6, 10), (10, 14)]
OWN = 14
XF = 1
KD, KG = 6, 3
NT = 6
BIG = float(2 ** 26)

_f, _b, _h, _i, _u = "float32", "bfloat16", "float16", "int32", "uint16"
SCRATCH = {
    "featW": ("sbuf", [128, 2 * W], _b), "kidi": ("sbuf", [128, W], _i), "kid": ("sbuf", [128, W + 16], _f),
    "keyW": ("sbuf", [128, W], _f), "idW": ("sbuf", [128, W + 16], _f),
    "Wx": ("sbuf", [128, W], _b), "D": ("sbuf", [128, W], _b), "A": ("sbuf", [128, 16, 256], _b), "raw": ("sbuf", [128, 512], _b),
    "LH": ("sbuf", [128, 2048], _b), "SH": ("sbuf", [128, 2048], _h), "R16": ("sbuf", [128, 8, 32], _h),
    "i1": ("sbuf", [128, 128], _i), "i1b": ("sbuf", [128, 128], _i), "i2": ("sbuf", [128, 16], _i), "i2b": ("sbuf", [128, 16], _i),
    "i3": ("sbuf", [128, 16], _i), "i3b": ("sbuf", [128, 16], _i), "i4": ("sbuf", [128, 16], _i), "i5": ("sbuf", [128, 16], _i), "i6": ("sbuf", [128, 16], _i),
    "bi": ("sbuf", [128, 16], _i), "exb": ("sbuf", [128, 16], _u), "dg": ("sbuf", [128, 16], _f), "ib": ("sbuf", [128, 8], _i),
    "a1": ("sbuf", [128, 16], _f), "a2": ("sbuf", [128, 16], _f), "a3": ("sbuf", [128, 16], _f), "a4": ("sbuf", [128, 16], _f),
    "blk": ("sbuf", [128, 128], _f), "diag": ("sbuf", [128, 256], _f), "I16": ("sbuf", [128, 128], _h), "IB": ("sbuf", [128, 128], _b),
    "IN": ("sbuf", [128, 128], _b), "If": ("sbuf", [128, 128], _f), "ones": ("sbuf", [128, 128], _b), "wblk": ("sbuf", [128, 128], _b),
    "b8": ("sbuf", [128, 8], _b), "Kc": ("sbuf", [128, 256], _b), "expl": ("sbuf", [128, 16], _u),
    "RST": ("sbuf", [128, 256], _f), "RZ": ("sbuf", [128, 256], _f), "R1": ("sbuf", [128, 256], _f), "R2": ("sbuf", [128, 256], _f),
    "CJ": ("sbuf", [128, 16], _f), "CJ2": ("sbuf", [128, 256], _f),
    "col": ("sbuf", [128, 16], _f), "offc": ("sbuf", [128, 16], _f), "wti": ("sbuf", [128, 1], _i), "wtf": ("sbuf", [128, 1], _f),
    "ci": ("sbuf", [128, 256], _i), "mkb": ("sbuf", [128, 256], _b), "moi": ("sbuf", [128, 256], _i), "mk16": ("sbuf", [128, 256], _h), "mo16": ("sbuf", [128, 256], _h),
    "lai": ("sbuf", [128, 16], _i), "LX": ("sbuf", [128, 32], _f), "LT": ("sbuf", [128, 32], _f), "prev0": ("sbuf", [128, 16], _f),
    "X": ("sbuf", [128, 16, 32], _h), "XT": ("sbuf", [128, 16, 32], _h), "Y": ("sbuf", [128, 16, 32], _h), "YT": ("sbuf", [128, 16, 32], _h),
    "G": ("sbuf", [128, 8, 32], _h), "GT": ("sbuf", [128, 8, 32], _h), "PM": ("sbuf", [128, 512], _h), "S4": ("sbuf", [128, 4, 2, 16], _h),
    "MK": ("sbuf", [128, 256], _f), "Lp": ("sbuf", [128, 256], _f), "vm": ("sbuf", [128, 256], _f), "vI": ("sbuf", [128, 256], _i),
    "oa": ("sbuf", [128, 16], _i), "kk": ("sbuf", [128, 16], _i), "po": ("sbuf", [128, 16], _i), "pb": ("sbuf", [128, 16], _i), "pbb": ("sbuf", [128, 16], _i), "pu": ("sbuf", [128, 16], _u),
    "ky": ("sbuf", [128, 256], _f), "ks": ("sbuf", [128, 256], _i), "key": ("sbuf", [128, 16], _i),
    "eq": ("sbuf", [128, 256], _f), "em": ("sbuf", [128, 256], _f), "es": ("sbuf", [128, 256], _i),
    "eo": ("sbuf", [128, 16], _i), "sT": ("sbuf", [128, 16], _i), "sL": ("sbuf", [128, 16], _i), "de": ("sbuf", [128, 16], _i),
    "tT": ("sbuf", [128, 16], _i), "tL": ("sbuf", [128, 16], _i), "l2": ("sbuf", [128, 32], _i), "u2": ("sbuf", [128, 32], _u),
    "top": ("sbuf", [128, 256], _f), "cf": ("sbuf", [128, 256], _f),
    "na": ("sbuf", [128, 16], _f), "cov": ("sbuf", [128, 16], _b), "ncd": ("sbuf", [128, 16], _f), "s1": ("sbuf", [128, 16], _f), "s1u": ("sbuf", [128, 16], _u),
    "gl": ("sbuf", [128, 256], _f), "eq2": ("sbuf", [128, 256], _f), "dsum": ("sbuf", [128, 256], _f), "dd": ("sbuf", [128, 16], _f), "s2": ("sbuf", [128, 16], _f), "s2u": ("sbuf", [128, 32], _u),
    "dk": ("sbuf", [128, 16], _f), "dk2": ("sbuf", [128, 16], _f), "pn": ("sbuf", [128, 16], _f), "dn": ("sbuf", [128, 16], _f), "dn2": ("sbuf", [128, 16], _f),
    "cs": ("sbuf", [128, 1], _f), "csi": ("sbuf", [128, 1], _i), "csa": ("sbuf", [128, 1], _i), "limA": ("sbuf", [128, 1], _f),
    "yno": ("sbuf", [128, 256], _f), "ymo": ("sbuf", [128, 256], _f), "acc": ("sbuf", [128, 512], _f),
    "outC": ("sbuf", [128, STEPS * 272], _u), "inC": ("sbuf", [128, (STEPS + 1) * 272], _u),
    "outW": ("sbuf", [128, STEPS * 256], _b), "inW": ("sbuf", [128, STEPS * 256], _b),
    "pv": ("psum", [128, 8, 32], _f), "pL": ("psum", [128, 8, 32], _f), "pM": ("psum", [128, 512], _f), "pC": ("psum", [128, 512], _f),
    "pW": ("psum", [128, 512], _f), "pA": ("psum", [128, 512], _f), "pB": ("psum", [128, 512], _f), "pX": ("psum", [128, 512], _f),
}
DMAS = ["cand", "want", "wts", "last", "mkey", "mobj", "f0", "fd", "k0", "k1", "k2", "k3", "yn", "ymu", "yd"]
SEMAPHORES = ["sv", "st", "ss", "sg", "ls"] + ["d_" + n for n in DMAS] + ["w%d" % t for t in range(1, STEPS)] + [x + "%d" % t for t in range(1, STEPS + 1) for x in "ab"]


def make(g, T):
    Q = {"v": g.vector, "t": g.tensor, "s": g.scalar, "g": g, "y": g.sync}
    own = {"v": "sv", "t": "st", "s": "ss", "g": "sg"}
    cnt, known, hist, tags = {}, {q: {} for q in Q}, {}, {}

    def tag(n):
        if n not in tags:
            tags[n] = {"w": {}, "r": {}, "base": {}, "full": False}
        return tags[n]

    def merge(a, b):
        for s, c in b.items():
            if a.get(s, 0) < c:
                a[s] = c

    def wait(q, needs):
        for s in sorted(needs, key=lambda s: -len(hist.get((s, needs[s]), {}))):
            c = needs[s]
            if known[q].get(s, 0) < c:
                Q[q].wait_ge(T.sem[s], c)
                merge(known[q], hist.get((s, c), {}))
                merge(known[q], {s: c})

    def deps(q, r, w, p, acc):
        need = {}
        for n in r:
            merge(need, tag(n)["w"])
        for n in w:
            d = tag(n)
            for m in (d["w"], d["r"], d["base"]):
                merge(need, {s: c for s, c in m.items() if not (acc and s == own.get(q))})
        for n in p:
            d = tag(n)
            if d["full"] or d["r"]:
                merge(d["base"], d["w"])
                merge(d["base"], d["r"])
                d["w"], d["r"], d["full"] = {}, {}, False
            merge(need, d["base"])
        return need

    def mark(s, c, r, w, p, acc):
        for n in r:
            merge(tag(n)["r"], {s: c})
        for n in w:
            if acc:
                merge(tag(n)["w"], {s: c})
                tag(n)["r"] = {}
            else:
                tags[n] = {"w": {s: c}, "r": {}, "base": {}, "full": True}
        for n in p:
            merge(tag(n)["w"], {s: c})

    def op(q, fn, args, r=(), w=(), p=(), acc=False, kw=None):
        wait(q, deps(q, r, w, p, acc))
        s = own[q]
        cnt[s] = c = cnt.get(s, 0) + 1
        fn(*args, **(kw or {})).then_inc(T.sem[s], 1)
        hist[(s, c)] = dict(known[q])
        mark(s, c, r, w, p, acc)

    def dma(q, out, in_, name, r=(), w=(), p=()):
        wait(q, deps(q, r, w, p, False))
        s = "d_" + name
        cnt[s] = 16
        Q[q].dma_start(out, in_).then_inc(T.sem[s], 16)
        hist[(s, 16)] = dict(known[q])
        mark(s, 16, r, w, p, False)

    def arrive(s, c, w):
        cnt[s] = c
        mark(s, c, (), w, (), False)

    def need(q, r):
        wait(q, deps(q, r, (), (), False))

    def finish(q):
        for s in sorted(cnt):
            if known[q].get(s, 0) < cnt[s]:
                Q[q].wait_ge(T.sem[s], cnt[s])
    return op, dma, arrive, need, finish, cnt


def rank_program(g, core, T, topo):
    rank = T.rank_of(core)
    if rank is None:
        return
    op, dma, arrive, need, finish, cnt = make(g, T)
    v, te, sc = g.vector, g.tensor, g.scalar
    n = len(T.cores)
    nxt, prv = T.cores[(rank + 1) % n], T.cores[(rank - 1) % n]
    rid, pid, _se = topo.addr(nxt)
    mask, nout, nin = topo.mask(core, nxt), len(topo.engines(core, nxt)), len(topo.engines(prv, core))

    def ts(out, in0, s1, s2, o0, o1, r, w=(), p=()):
        args = (out, in0, s1, s2, o0) if o1 is None else (out, in0, s1, s2, o0, o1)
        op("v", v.tensor_scalar, args, r, w, p)

    def tt(out, a, b, o, r, w=(), p=()):
        op("v", v.tensor_tensor, (out, a, b, o), r, w, p)

    def cp(out, a, r, w=(), p=()):
        op("v", v.tensor_copy, (out, a), r, w, p)

    def scan(out, d0, d1, o0, o1, r, w):
        op("v", v.tensor_tensor_scan, (out, d0, d1, 0.0, o0, o1), r, (w,))

    def act(out, a, f, r, w=(), p=(), **kw):
        op("s", sc.activation, (out, a, f), r, w, p, kw=kw)

    def mm(out, l, rh, st, sp, r, w):
        op("t", te.matmul, (out, l, rh, st, sp), r, (w,), acc=not st)

    def send(out, in_, sem, r):
        need("g", r)
        g.remote_dma(out, in_, T.sem[sem], T.sem.ls, pid, rid, mask)
        cnt["ls"] = cnt.get("ls", 0) + nout

    def fill(ap, x, w=(), p=()):
        op("v", v.memset, (ap, x), (), w, p)

    def iota(out, pat, base, ch, w, **kw):
        op("g", g.iota, (out, pat, base, ch), (), (w,), kw=kw)
    C = lambda j: T.col[:, j:j + 1]
    M1, M0, SCT, BIT, CEN, DUMP, THR, OFF, CEN0 = range(9)
    inC = lambda t: T.inC[:, 272 * t:272 * t + 256]
    inP = lambda t: T.inC[:, 272 * t + 256:272 * t + 272]
    outO = lambda t: T.outC[:, 272 * t + 256:272 * t + 272]
    inW = lambda t: T.inW[:, 256 * t:256 * t + 256]
    outW = lambda t: T.outW[:, 256 * t:256 * t + 256]
    last16 = lambda b: b[:, 15::16]

    dma("s", T.ci[:], T.cand[:], "cand", w=("ci",))
    dma("y", inW(0), T.want[:], "want", w=("inW0",))
    dma("y", T.featW[:, 0:W], T.feat[:], "f0", w=("feat",))
    dma("s", T.mkb[:], T.mkey[:], "mkey", w=("mkb",))
    dma("s", T.moi[:], T.mobj[:], "mobj", w=("moi",))
    dma("s", T.wti[:], T.wts[:], "wts", w=("wti",))
    dma("s", T.lai[:], T.last[:], "last", w=("lai",))
    for q in range(4):
        dma("y", T.kidi[:, 1024 * q:1024 * q + 1024], T.kids[:, 1024 * q:1024 * q + 1024], "k%d" % q, w=("kidi%d" % q,))
    dma("y", T.featW[:, W:2 * W], T.feat[:], "fd", w=("featd",))

    iota(T.i5[:], [[0, 16]], 0, 1, "i5")
    iota(T.i2[:], [[1, 16]], 128, -1, "i2")
    iota(T.i1[:], [[16, 8], [0, 16]], 15, -1, "i1")
    iota(T.i4[:], [[1, 16]], 0, 0, "i4")
    iota(T.i3[:], [[1, 16]], 0, 1, "i3")
    iota(T.i6[:], [[256, 16]], 0, 0, "i6")
    iota(T.Kc[:], [[0, 16], [4096, 16]], 2048, 0, "Kc", allow_small_or_imprecise_dtypes=True)
    iota(T.idW[:], [[1, W + 16]], 0, 0, "idW", allow_small_or_imprecise_dtypes=True)
    fill(T.LH[:], 0.0, w=("LH",))
    ts(T.i2b[:], T.i2[:], 15, None, ALU.bitwise_and, None, ("i2",), ("i2b",))
    ts(T.bi[:], T.i5[:], 15, None, ALU.bitwise_and, None, ("i5",), ("bi",))
    ts(T.i1b[:], T.i1[:], 4, None, ALU.arith_shift_right, None, ("i1",), ("i1b",))
    ts(T.ib[:, 0:1], T.i5[:, 0:1], 4, 1, ALU.logical_shift_right, ALU.bitwise_and, ("i5",), ("ib0",))
    ts(T.ib[:, 1:2], T.i5[:, 0:1], 3, 1, ALU.logical_shift_right, ALU.bitwise_and, ("i5",), ("ib1",))
    ts(T.dg[:], T.i2b[:], 0.0, None, ALU.is_equal, None, ("i2b",), ("dg",))
    cp(T.exb[:], T.bi[:], ("bi",), ("exb",))
    ts(T.blk[:], T.i1b[:], 0.0, None, ALU.is_equal, None, ("i1b",), ("blk",))
    act(T.diag[:], T.dg[:].indirect(T.exb[:]), AF.Copy, ("dg", "exb"), ("diag",))
    ts(T.b8[:], T.blk[:, 0::16], 65536.0, None, ALU.mult, None, ("blk",), ("b8",))
    cp(C(M1), T.ib[:, 0:1], ("ib0",), ("m1",))
    ts(C(M0), T.ib[:, 0:1], -1.0, 1.0, ALU.mult, ALU.add, ("ib0",), ("m0",))
    ts(C(SCT), T.ib[:, 1:2], -1.0, 1.0, ALU.mult, ALU.add, ("ib1",), ("sct",))
    ts(C(DUMP), T.bi[:, 0:1], float(W), None, ALU.add, None, ("bi",), ("dump",))
    fill(C(CEN0), 2048.0, w=("cen0",))
    for b in range(16):
        act(T.LH[:, 129 * b:129 * b + 113:16], T.b8[:], AF.Copy, ("b8",), p=("LH",))
    tt(T.If[:], T.blk[:], T.diag[:, 0:128], ALU.mult, ("blk", "diag"), ("If",))
    cp(T.inC[:, 0:256], T.ci[:], ("ci",), ("inCa0", "inCb0"))
    cp(T.I16[:], T.If[:], ("If",), ("I16",))
    cp(T.IB[:], T.If[:], ("If",), ("IB",))
    ts(T.IN[:], T.If[:], -1.0, None, ALU.mult, None, ("If",), ("IN",))

    def expand(t, q, k):
        out, nm = T.Wx[:, k::16], "inW%d" % t
        if q == "v":
            cp(out, inW(t), (nm,), p=("Wx",))
        elif q == "s":
            act(out, inW(t), AF.Copy, (nm,), p=("Wx",))
        else:
            op("g", g.affine_select, (out, inW(t), [[0, 256]], ALU.is_equal, 0.0, 0, 0), (nm,), p=("Wx",))
    for k in range(16):
        expand(0, "v" if k < KD else "s", k)
    cp(T.wtf[:], T.wti[:], ("wti",), ("wtf",))
    ts(T.wblk[:], T.blk[:], T.wtf[:], None, ALU.mult, None, ("blk", "wtf"), ("wblk",))
    fill(T.R1[:], 1.0, w=("R1",))
    fill(T.R1[:, 0::16], 0.0, p=("R1",))
    act(T.R2[:], T.R1[:], AF.Copy, ("R1",), ("R2",), scale=2.0)
    act(T.RZ[:], T.R1[:], AF.Copy, ("R1",), ("RZ",), scale=BIG)
    act(T.RST[:], T.R1[:], AF.Copy, ("R1",), ("RST",), scale=-BIG, bias=BIG)
    ts(C(BIT), C(SCT), 4097.0, -1.0, ALU.mult, ALU.add, ("sct",), ("bit",))
    ts(C(CEN), C(SCT), 4096.0, 2048.0, ALU.mult, ALU.add, ("sct",), ("cen",))
    ts(C(OFF), C(SCT), 4096.0, None, ALU.mult, None, ("sct",), ("off",))
    cp(T.expl[:], T.i4[:], ("i4",), ("expl",))
    fill(T.limA[:], 65536.0 * (LIM - 1), w=("limA",))
    ts(T.pbb[:], T.bi[:], 16.0, None, ALU.mult, None, ("bi",), ("pbb",))
    ts(T.i3b[:], T.i3[:], 15, None, ALU.bitwise_and, None, ("i3",), ("i3b",))
    tt(T.pb[:], T.pbb[:], T.i6[:], ALU.add, ("pbb", "i6"), ("pb",))
    ts(T.a1[:], T.i3b[:], -16384.0, 262144.0 + 4096.0, ALU.mult, ALU.add, ("i3b",), ("a1",))
    ts(T.a2[:], T.i3b[:], 10.0, 4096.0, ALU.is_lt, ALU.mult, ("i3b",), ("a2",))
    ts(T.a3[:], T.i3b[:], 4.0, 4096.0, ALU.is_lt, ALU.mult, ("i3b",), ("a3",))
    tt(T.a4[:], T.a1[:], T.a2[:], ALU.add, ("a1", "a2"), ("a4",))
    tt(T.CJ[:], T.a4[:], T.a3[:], ALU.add, ("a4", "a3"), ("CJ",))
    act(T.CJ2[:], T.CJ[:].indirect(T.exb[:]), AF.Copy, ("CJ", "exb"), ("CJ2",), bias=2048.0)
    cp(T.R16[:, :, 0:16], T.I16[:], ("I16",), p=("R16",))
    cp(T.R16[:, :, 16:32], T.I16[:], ("I16",), p=("R16",))
    for s in range(2):
        cp(T.S4[:, :, s, :], T.R16[:, 1 - s::2, 0:16], ("R16",), p=("S4",))
    for e, m, nm in ((0, M0, "m0"), (1, M1, "m1")):
        ts(T.PM[:, 384 * e:384 * e + 128], T.I16[:], C(m), None, ALU.mult, None, ("I16", nm), p=("PM",))
        ts(T.PM[:, 128 + 128 * e:256 + 128 * e], T.S4[:], C(m), None, ALU.mult, None, ("S4", nm), p=("PM",))
    for b in range(16):
        cp(T.SH[:, 128 * b:128 * b + 128], T.R16[:, :, b:b + 16], ("R16",), p=("SH",))

    def flip_calls(src, ns, X, XT, nx):
        return [lambda: ts(X[:, :, 0:16], src, C(M0), None, ALU.mult, None, (ns, "m0"), p=(nx,)),
                lambda: ts(X[:, :, 16:32], src, C(M1), None, ALU.mult, None, (ns, "m1"), p=(nx,)),
                lambda: op("v", v.transpose, (XT[:], X[:]), (nx,), (nx + "T",))]

    def halves(out, XT, nx, w):
        mm(out, T.I16[:], XT[:, :, 0:16], True, False, ("I16", nx + "T"), w)
        mm(out, T.I16[:], XT[:, :, 16:32], False, True, ("I16", nx + "T"), w)
    cp(T.mk16[:], T.mkb[:], ("mkb",), ("mk16",))
    ts(T.mo16[:], T.moi[:], 2048.0, None, ALU.subtract, None, ("moi",), ("mo16",))
    for ps, src in (("pA", "mk16"), ("pB", "mo16")):
        for b in range(16):
            op("t", te.matmul, (T[ps][:, b:256:16], T.SH[:, 128 * b:128 * b + 128], T[src][:, b::16], True, True), ("SH", src), p=(ps,))
    for f in flip_calls(T.pA[:, 0:256], "pA", T.X, T.XT, "X") + flip_calls(T.pB[:, 0:256], "pB", T.Y, T.YT, "Y"):
        f()
    halves(T.pA[:, 0:256], T.XT, "X", "pA")
    halves(T.pB[:, 0:256], T.YT, "Y", "pB")
    ts(T.LX[:, 0:16], T.lai[:], C(M0), None, ALU.mult, None, ("lai", "m0"), p=("LX",))
    ts(T.LX[:, 16:32], T.lai[:], C(M1), None, ALU.mult, None, ("lai", "m1"), p=("LX",))
    op("v", v.transpose, (T.LT[:], T.LX[:]), ("LX",), ("LT",))
    tt(T.prev0[:], T.LT[:, 0:16], T.LT[:, 16:32], ALU.add, ("LT",), ("prev0",))
    scan(T.dsum[:], T.R2[:], T.diag[:], ALU.mult, ALU.add, ("R2", "diag"), "dsum")
    ts(C(THR), T.dsum[:, 15:16], 2.0, None, ALU.mult, None, ("dsum",), ("thr",))
    ts(T.offc[:], T.dg[:], 0.0, C(OFF), ALU.mult, ALU.add, ("dg", "off"), ("offc",))
    act(T.MK[:], T.pA[:, 0:256], AF.Copy, ("pA",), ("MK",))
    tt(T.pM[:, 0:256], T.pB[:, 0:256], T.CJ2[:], ALU.add, ("pB", "CJ2"), ("pM",))
    fill(T.ones[:], 1.0, w=("ones",))

    kbank = ["pC", "pW", "pA", "pB"]

    def keys(i0):
        for i in range(i0, i0 + 4):
            p = kbank[i % 4]
            mm(T[p][:], T.wblk[:], T.featW[:, 512 * i:512 * i + 512], True, True, ("wblk", "feat"), p)
        for i in range(i0, i0 + 4):
            p = kbank[i % 4]
            act(T.keyW[:, 512 * i:512 * i + 512], T[p][:], AF.Copy, (p,), p=("keyW",))

    scq = []

    def scatters():
        scq.extend(range(15, -1, -1))

    def scatter(k=1):
        for i in range(min(k, len(scq))):
            c = scq.pop(0)
            tt(T.kid[:].indirect(T.s2u[:, 2 * c:2 * c + 1]), T.cf[:, 16 * c:16 * c + 16], T.offc[:], ALU.subtract, ("s2u", "cf0", "cf1", "offc"), ("kid",))

    def limit():
        mm(T.pC[:, 0:16], T.ones[:], T.cov[:], True, True, ("ones", "cov"), "pC")
        return [lambda: op("v", v.tensor_reduce, (T.cs[:], T.pC[:, 0:16], AxisListType.X, ALU.add), ("pC",), ("cs",), kw=dict(negate=True)),
                lambda: cp(T.csi[:], T.cs[:], ("cs",), ("csi",)),
                lambda: ts(T.csa[:], T.csi[:], 15, None, ALU.bitwise_and, None, ("csi",), ("csa",)),
                lambda: ts(T.limA[:], T.csa[:], 65536.0, 65536.0 * (LIM - 1), ALU.mult, ALU.add, ("csa",), ("limA",))]

    def dist(c0, c1, nm, stop):
        for b in range(16):
            mm(T.pv[:, c0 // 2:c1 // 2, :], T.LH[:, 128 * b:128 * b + 128], T.A[:, c0:c1, 16 * b:16 * b + 16], False, stop and b == 15, ("LH", nm), "pv")
    keys(0)
    for t in range(STEPS):
        iw, ia, ibn, final = "inW%d" % t, "inCa%d" % t, "inCb%d" % t, t == STEPS - 1
        fw = 2 * W if t else W
        fr = ("feat", "featd") if t else ("feat",)
        mm(T.pv[:], T.IB[:], T.Kc[:], True, False, ("IB", "Kc"), "pv")
        mm(T.pL[:], T.IB[:], T.Kc[:], True, False, ("IB", "Kc"), "pL")
        for x, (c0, c1) in enumerate(CH):
            tt(T.D[:, 256 * c0:256 * c1], T.featW[:, 0:fw].indirect(T.inC[:, 272 * t + 16 * c0:272 * t + 16 * c1]), T.Wx[:, 256 * c0:256 * c1], ALU.subtract,
               fr + ("Wx", ia) + ((ibn,) if c1 > 8 else ()), ("D%d" % x,))
            if x == XF:
                ts(T.G[:], inC(t), C(CEN if t else CEN0), None, ALU.subtract, None, (ia, ibn, "cen" if t else "cen0"), ("G",))
                scatter()
                op("v", v.transpose, (T.GT[:], T.G[:]), ("G",), ("GT",))
            if x == 0:
                act(T.raw[:], T.featW[:, 0:fw].indirect(T.inC[:, 272 * t + 16 * OWN:272 * t + 256]), AF.Copy, fr + (ibn,), ("raw",))
                mm(T.pX[:], T.IB[:], T.raw[:], True, False, ("IB", "raw"), "pX")
                mm(T.pX[:], T.IN[:], T.Wx[:, 256 * OWN:4096], False, True, ("IN", "Wx"), "pX")
            act(T.A[:, c0:c1, :], T.D[:, 256 * c0:256 * c1], AF.Abs, ("D%d" % x,), ("A%d" % x,))
            if x == 1:
                act(T.A[:, OWN:16, :], T.pX[:], AF.Abs, ("pX",), ("A9",))
            if x == 2:
                act(T.Lp[:], T.pL[:], AF.Identity, ("pL", "limA"), ("Lp",), bias=T.limA[:])
            if x == len(CH) - 1 and not final:
                act(T.D[:, 256 * OWN:4096], T.pX[:], AF.Abs, ("pX",), ("D9",))
            if x == XF:
                for p, e in (("pL", True), ("pv", False)):
                    for c in range(2):
                        for s in range(2):
                            o = 256 * c + 128 * s
                            mm(T[p][:, :, 16 * c:16 * c + 16], T.PM[:, o:o + 128], T.GT[:, :, 16 * s:16 * s + 16], False, e and c + s == 2, ("PM", "GT"), p)
            dist(c0, c1, "A%d" % x, x == len(CH) - 1)
            if x == 1:
                dist(OWN, 16, "A9", False)
        if t == 0:
            keys(4)
            for q in range(4):
                cp(T.kid[:, 1024 * q:1024 * q + 1024], T.kidi[:, 1024 * q:1024 * q + 1024], ("kidi%d" % q,), p=("kid",))
        else:
            scatter(NT)
        tt(T.vm[:], T.pv[:], T.Lp[:], ALU.max, ("pv", "Lp"), ("vm",))
        scatter()
        scan(T.vI[:], T.RST[:], T.vm[:], ALU.max, ALU.min, ("RST", "vm"), "vI")
        scatter()
        ts(T.oa[:], last16(T.vI), 4095, None, ALU.bitwise_and, None, ("vI",), ("oa",))
        oo = "outO%d" % t
        if not final:
            ts(T.kk[:], last16(T.vI), 12, 15, ALU.logical_shift_right, ALU.bitwise_and, ("vI",), ("kk",))
        scatter()
        cp(outO(t), T.oa[:], ("oa",), (oo,))
        if not final:
            tt(T.po[:], T.kk[:], T.pb[:], ALU.add, ("kk", "pb"), ("po",))
        scatter()
        tt(T.ky[:], T.keyW[:].indirect(outO(t)), T.diag[:], ALU.mult, ("keyW", oo, "diag"), ("ky",))
        if not final:
            cp(T.pu[:], T.po[:], ("po",), ("pu",))
            act(outW(t), T.D[:].indirect(T.pu[:]), AF.Abs, tuple("D%d" % x for x in range(len(CH))) + ("D9", "pu"), ("outW%d" % t,))
            send(inW(t + 1), outW(t), "w%d" % (t + 1), ("outW%d" % t,))
        scatter()
        scan(T.ks[:], T.R1[:], T.ky[:], ALU.mult, ALU.add, ("R1", "ky"), "ks")
        scatter()
        ts(T.key[:], last16(T.ks), 63, None, ALU.bitwise_and, None, ("ks",), ("key",))
        scatter()
        tt(T.eq[:], T.key[:].indirect(T.expl[:]), T.MK[:], ALU.is_equal, ("key", "expl", "MK"), ("eq",))
        scatter()
        tt(T.em[:], T.eq[:], T.pM[:, 0:256], ALU.mult, ("eq", "pM"), ("em",))
        scatter()
        scan(T.es[:], T.RZ[:], T.em[:], ALU.min, ALU.max, ("RZ", "em"), "es")
        scatter(16)
        ev = last16(T.es)
        ts(T.eo[:], ev, 4095, None, ALU.bitwise_and, None, ("es",), ("eo",))
        ts(T.sT[:], ev, 13, 1, ALU.logical_shift_right, ALU.bitwise_and, ("es",), ("sT",))
        ts(T.sL[:], ev, 12, 1, ALU.logical_shift_right, ALU.bitwise_and, ("es",), ("sL",))
        tt(T.de[:], T.eo[:], T.oa[:], ALU.subtract, ("eo", "oa"), ("de",))
        q = 5 * t % 16
        pr, prn = (inP(t), ibn) if t else (T.prev0[:], "prev0")
        ts(T.ncd[:], ev, 1.0, C(DUMP), ALU.is_lt, ALU.mult, ("es", "dump"), ("ncd",))
        tt(T.dk[:], T.key[:], T.MK[:, q::16], ALU.subtract, ("key", "MK"), ("dk",))
        tt(T.tT[:], T.sT[:], T.de[:], ALU.mult, ("sT", "de"), ("tT",))
        tt(T.tL[:], T.sL[:], T.de[:], ALU.mult, ("sL", "de"), ("tL",))
        ts(T.pn[:], pr, T.CJ[:, q:q + 1], None, ALU.add, None, (prn, "CJ"), ("pn",))
        ts(T.na[:], last16(T.vI), T.limA[:], 65536.0, ALU.subtract, ALU.is_ge, ("vI", "limA"), ("na",))
        tt(T.l2[:, 0:16], T.tT[:], T.oa[:], ALU.add, ("tT", "oa"), p=("l2",))
        tt(T.l2[:, 16:32], T.tL[:], T.oa[:], ALU.add, ("tL", "oa"), p=("l2",))
        tt(T.s1[:], T.oa[:], T.ncd[:], ALU.max, ("oa", "ncd"), ("s1",))
        tt(T.dk2[:], T.dk[:], T.na[:], ALU.mult, ("dk", "na"), ("dk2",))
        cp(T.u2[:], T.l2[:], ("l2",), ("u2",))
        for h in range(2):
            act(T.top[:, 128 * h:128 * h + 128], T.kid[:, 0:W].indirect(T.u2[:, 8 * h:8 * h + 8]), AF.Identity, ("kid", "u2", "sct", "bit"), ("top%d" % h,),
                bias=C(BIT), scale=C(SCT))
        tt(T.dn[:], T.pn[:], T.pM[:, q:256:16], ALU.subtract, ("pn", "pM"), ("dn",))
        cp(T.s1u[:], T.s1[:], ("s1",), ("s1u",))
        tt(T.MK[:, q::16], T.MK[:, q::16], T.dk2[:], ALU.add, ("dk2",), ("MK",))
        tt(T.dn2[:], T.dn[:], T.na[:], ALU.mult, ("dn", "na"), ("dn2",))
        for h in range(2):
            s = slice(128 * h, 128 * h + 128)
            tt(T.cf[:, s], T.kid[:, 0:W].indirect(T.u2[:, 16 + 8 * h:24 + 8 * h]), T.top[:, s], ALU.max, ("kid", "u2", "top%d" % h), ("cf%d" % h,))
        for h in range(2):
            o = 272 * t + 128 * h
            e = o + (144 if h and not final else 128)
            if h:
                tt(T.pM[:, q:256:16], T.dn2[:], T.pM[:, q:256:16], ALU.add, ("dn2",), ("pM",))
            cp(T.outC[:, o:o + 128], T.cf[:, 128 * h:128 * h + 128], ("cf%d" % h,), ("oC%d" % h,))
            send(T.inC[:, o + 272:e + 272], T.outC[:, o:e], "ab"[h] + "%d" % (t + 1), ("oC%d" % h, oo))
        if not final:
            act(T.cov[:], T.ncd[:], AF.Sign, ("ncd",), ("cov",))
        act(T.gl[:], T.idW[:].indirect(T.s1u[:]), AF.Copy, ("idW", "s1u"), ("gl",))
        lim, wq = [], []
        if not final:
            lim = limit()
            arrive("w%d" % (t + 1), nin, ("inW%d" % (t + 1),))
            arrive("a%d" % (t + 1), nin, ("inCa%d" % (t + 1),))
            arrive("b%d" % (t + 1), nin, ("inCb%d" % (t + 1),))
            for k in range(KD, 16):
                expand(t + 1, "s" if k < 16 - KG else "g", k)
            wq = list(range(KD))
        def fill_in():
            if lim:
                lim.pop(0)()
            if wq:
                expand(t + 1, "v", wq.pop(0))
        fill_in()
        tt(T.eq2[:], T.s1[:].indirect(T.expl[:]), T.gl[:], ALU.is_equal, ("s1", "expl", "gl"), ("eq2",))
        fill_in()
        scan(T.dsum[:], T.R2[:], T.eq2[:], ALU.mult, ALU.add, ("R2", "eq2"), "dsum")
        fill_in()
        ts(T.dd[:], last16(T.dsum), C(THR), C(DUMP), ALU.is_ge, ALU.mult, ("dsum", "thr", "dump"), ("dd",))
        fill_in()
        tt(T.s2[:], T.s1[:], T.dd[:], ALU.max, ("s1", "dd"), ("s2",))
        fill_in()
        cp(T.s2u[:, 0::2], T.s2[:], ("s2",), ("s2u",))
        scatters()
        while wq:
            fill_in()
        if not final:
            scatter()
    calls = [lambda: tt(T.mo16[:], T.pM[:, 0:256], T.CJ2[:], ALU.subtract, ("pM", "CJ2"), ("mo16",)),
             lambda: ts(T.mk16[:], T.MK[:], 1.0 / 64, None, ALU.mult, None, ("MK",), ("mk16",))]
    for f in calls + flip_calls(T.mo16[:], "mo16", T.X, T.XT, "X") + flip_calls(T.mk16[:], "mk16", T.Y, T.YT, "Y"):
        scatter()
        f()
    for b in range(16):
        sh = T.SH[:, 128 * (-b % 16):128 * (-b % 16) + 128]
        for e, (XT, nx, o) in enumerate(((T.XT, "XT", 0), (T.XT, "XT", 16), (T.YT, "YT", 0), (T.YT, "YT", 16))):
            op("t", te.matmul, (T.pA[:, b:256:16], sh, XT[:, :, o + b], e == 0, e == 3), ("SH", nx), p=("pA",))
    scatter(16)
    yb = ["pB", "pC", "pW", "pX"]
    for i in range(1, 5):
        act(T[yb[i - 1]][:], T.kid[:, 512 * i:512 * i + 512], AF.Copy, ("kid",), (yb[i - 1],), scale=float(i + 1))
    arrive("a%d" % STEPS, nin, ("inCa%d" % STEPS,))
    arrive("b%d" % STEPS, nin, ("inCb%d" % STEPS,))
    tt(T.acc[:], T.kid[:, 0:512], T[yb[0]][:], ALU.add, ("kid", yb[0]), ("acc0", "acc1"))
    ts(T.yno[:], inC(STEPS), C(OFF), None, ALU.subtract, None, ("inCa%d" % STEPS, "inCb%d" % STEPS, "off"), ("yno",))
    dma("y", T.yn[:], T.yno[:], "yn", r=("yno",))
    act(T.ymo[:], T.pA[:, 0:256], AF.Copy, ("pA",), ("ymo",), scale=64.0, bias=131072.0)
    dma("s", T.ymu[:], T.ymo[:], "ymu", r=("ymo",))
    for i in range(2, 8):
        p = yb[(i - 1) % 4]
        if i > 4:
            act(T[p][:], T.kid[:, 512 * i:512 * i + 512], AF.Copy, ("kid",), (p,), scale=float(i + 1))
        for h in range(2):
            s, a = slice(256 * h, 256 * h + 256), "acc%d" % h
            tt(T.acc[:, s], T.acc[:, s], T[p][:, s], ALU.add, (a, p), (a,))
    dma("y", T.yd[:], T.acc[:], "yd", r=("acc0", "acc1"))
    finish("g")
